import numpy as np
import ml_dtypes


def mxq(x, axis, fmt="e4m3"):
    dtype, down = {"e4m3": (ml_dtypes.float8_e4m3fn, 7), "e5m2": (ml_dtypes.float8_e5m2, 14)}[fmt]
    v = np.moveaxis(np.asarray(x, np.float32).astype(ml_dtypes.bfloat16).astype(np.float64), axis, -1)
    blocks = v.reshape(v.shape[:-1] + (-1, 32))
    amax = np.abs(blocks).max(-1, keepdims=True)
    byte = np.maximum(np.where(amax > 0, np.frexp(amax)[1] - 1 + 127, 0) - down, 1)
    scale = np.exp2(byte - 127.0)
    codes = (blocks / scale).astype(np.float32).astype(dtype).astype(np.float64)
    return np.moveaxis((codes * scale).reshape(v.shape), -1, axis)


WIDE = False


def mx_kscale(k):
    if not WIDE:
        return np.ones(k)
    levels = np.array([10, -10, 5, -5, 0])
    if k % 512:
        return np.exp2(np.random.permutation(np.resize(levels, k // 32))).repeat(32)
    a = np.empty((k // 512, 16))
    for p in range(k // 512):
        a[p, :8] = np.random.permutation(np.resize(levels, 8))
        for g in range(8):
            far = levels[np.abs(levels - a[p, g]) >= 10]
            a[p, g + 8] = far[np.random.randint(len(far))]
    return np.exp2(a.ravel()).repeat(32)


BF16 = ml_dtypes.bfloat16


def bf(x):
    return np.asarray(x, np.float32).astype(BF16)


def f64(x):
    return np.asarray(x).astype(np.float64)


E2M1 = np.array([0.0, 0.5, 1.0, 1.5, 2.0, 3.0, 4.0, 6.0, -0.0, -0.5, -1.0, -1.5, -2.0, -3.0, -4.0, -6.0])


def pack_weight(w, fmt):
    k, n = w.shape
    w = f64(bf(w)).reshape(k // 32, 32, n)
    amax = np.abs(w).max(1)
    if fmt == "e4m3":
        byte = np.frexp(amax)[1] - 1 + 127 - 7
    else:
        mant, ex = np.frexp(amax / 6.0)
        byte = np.where(mant > 0.5, ex, ex - 1) + 127
    byte = np.clip(np.where(amax > 0, byte, 1), 1, 254)
    scaled = (w * np.exp2(127.0 - byte)[:, None, :]).reshape(k, n).astype(np.float32)
    by_word = np.ascontiguousarray(scaled.reshape(k // 512, 128, 4, n).transpose(0, 1, 3, 2))
    if fmt == "e4m3":
        words = by_word.astype(ml_dtypes.float8_e4m3fn).view(np.uint8)
    else:
        c = by_word.astype(ml_dtypes.float4_e2m1fn).view(np.uint8) & 0xF
        words = c[..., 0::2] | (c[..., 1::2] << 4)
    return np.ascontiguousarray(words), np.ascontiguousarray(byte.astype(np.uint8).reshape(k // 512, 16, n))


def unpack_weight(words, scales, fmt):
    g, p, n, _ = words.shape
    if fmt == "e4m3":
        vals = np.ascontiguousarray(words).view(ml_dtypes.float8_e4m3fn).astype(np.float64)
    else:
        nib = np.empty((g, p, n, 4), np.uint8)
        nib[..., 0::2] = words & 0xF
        nib[..., 1::2] = words >> 4
        vals = E2M1[nib]
    vals = vals * np.repeat(np.exp2(scales.astype(np.float64) - 127.0), 8, axis=1)[..., None]
    return vals.transpose(0, 1, 3, 2).reshape(g * 512, n)
def pack4(w):
    words, scales = pack_weight(w, "e2m1")
    return words.reshape(words.shape[0], 128, -1), scales


def unpack4(words, scales):
    return unpack_weight(words.reshape(words.shape[0], 128, -1, 2), scales, "e2m1")


def planes(Y):
    n, m = Y.shape
    b = f64(bf(Y)).reshape(n // 32, 32, m)
    amax = np.abs(b).max(1)
    byte = np.clip(np.where(amax > 0, np.frexp(amax)[1] - 1 + 127 - 7, 1), 1, 254)
    codes = (b * np.exp2(127.0 - byte)[:, None, :]).reshape(n, m).astype(np.float32).astype(ml_dtypes.float8_e4m3fn).view(np.uint8)
    words = codes.reshape(n // 512, 128, 4, m).transpose(0, 1, 3, 2)
    return np.ascontiguousarray(words), np.ascontiguousarray(byte.astype(np.uint8).reshape(n // 512, 16, m))


C, D, P, E, T = 1024, 1024, 1536, 512, 1024

def setup_inputs():
    s, u, t = mx_kscale(D), mx_kscale(E), mx_kscale(P)
    A = np.random.randn(D, C) * np.exp(0.3 * np.random.randn(C))[None, :] * s[:, None]
    B = np.random.randn(D, P) / np.sqrt(D) * t[None, :] / s[:, None]
    cand_words, cand_scales = pack_weight(A, "e4m3")
    pool_words, pool_scales = pack4(B)
    cover = bf((0.2 + 0.3 * np.abs(np.random.randn(P))) * t)
    item_desc = bf(np.random.randn(P, E) * u[None, :] / t[:, None])
    topic_map = bf(0.25 * np.random.randn(E, T) / np.sqrt(E) / u[:, None])
    item_bias = bf(0.1 * np.random.randn(P) / t)
    cost = bf(1 + 0.3 * np.random.randn(C))
    topic_scale = bf(0.3 * np.exp(0.8 * np.random.randn(T)))
    return {"cand_words": cand_words, "cand_scales": cand_scales, "pool_words": pool_words, "pool_scales": pool_scales,
            "cover": cover, "item_desc": item_desc, "topic_map": topic_map, "item_bias": item_bias,
            "cost": cost, "topic_scale": topic_scale}

def reference(cand_words, cand_scales, pool_words, pool_scales, cover, item_desc, topic_map, item_bias, cost, topic_scale):
    A = unpack_weight(cand_words, cand_scales, "e4m3")
    B = unpack4(pool_words, pool_scales)
    S = A.T @ B
    R = np.maximum(S - f64(cover)[None, :], 0.0)
    V = (mxq(f64(item_desc), 1, "e4m3") @ mxq(f64(topic_map), 0, "e4m3")) + f64(item_bias)[:, None]
    gain = mxq(R, 1, "e4m3") @ mxq(V, 0, "e4m3")
    y = (gain - f64(cost)[:, None]) * f64(topic_scale)[None, :]
    Y = y.T
    words, scales = planes(Y)
    return y, words, scales

@@ -1,0 +1,446 @@
+from contextlib import ExitStack
+
+import concourse.mybir as mybir
+from concourse.masks import make_identity
+
+F32 = mybir.dt.float32
+BF16 = mybir.dt.bfloat16
+U32 = mybir.dt.uint32
+I32 = mybir.dt.int32
+U8 = mybir.dt.uint8
+FP8X4 = mybir.dt.float8_e4m3fn_x4
+FP4X4 = mybir.dt.float4_e2m1fn_x4
+ACT = mybir.ActivationFunctionType
+ALU = mybir.AluOpType
+
+CANDS, EMB, POOL, DESC, TOPICS = 1024, 1024, 1536, 512, 1024
+FLOPS = 2 * CANDS * POOL * EMB + 2 * POOL * TOPICS * DESC + 2 * CANDS * TOPICS * POOL
+
+P = 128
+PACK = 4
+KPASS = P * PACK
+BANK = 512
+GROUPS = POOL // KPASS
+EMB_PASSES = EMB // KPASS
+CAND_TILES = CANDS // P
+CHUNKS = [(0, 256), (256, 768), (768, 1024)]
+LOADS = ["i0","b0","cv","t0","i1","bi","i2","b2","co","ts","bs","b1","a0","as","t2","t1","a1"]
+CAST_ON_SCALAR = {0: False, 1: True, 2: False}
+ORDER = [
+    ("item", 0, 0),
+    ("vec", 0),
+    ("bc", 1),
+    ("item", 0, 1),
+    ("map", 0),
+    ("bs",),
+    ("item", 1, 0),
+    ("item", 1, 1),
+    ("bc", 0),
+    ("vec", 1),
+    ("v", 0, 0, 0),
+    ("v", 0, 0, 2),
+    ("item", 2, 0),
+    ("item", 2, 1),
+    ("r", 0, 0, 0),
+    ("map", 1),
+    ("v", 0, 1, 0),
+    ("map", 2),
+    ("r", 0, 0, 1),
+    ("bc", 2),
+    ("v", 0, 1, 2),
+    ("r", 0, 0, 2),
+    ("v", 0, 2, 0),
+    ("r", 0, 1, 0),
+    ("r", 0, 0, 3),
+    ("r", 0, 2, 0),
+    ("r", 0, 2, 1),
+    ("r", 1, 1, 0),
+    ("r", 1, 1, 1),
+    ("r", 0, 2, 2),
+    ("r", 0, 2, 3),
+    ("v", 0, 2, 2),
+    ("r", 0, 1, 1),
+    ("r", 0, 1, 2),
+    ("r", 0, 1, 3),
+    ("r", 1, 1, 2),
+    ("r", 1, 0, 0),
+    ("r", 1, 0, 1),
+    ("r", 1, 2, 0),
+    ("r", 1, 1, 3),
+    ("r", 1, 0, 2),
+    ("v", 1, 2, 0),
+    ("v", 1, 0, 0),
+    ("r", 1, 0, 3),
+    ("v", 1, 0, 1),
+    ("v", 1, 0, 2),
+    ("gain", 0, 0),
+    ("gain", 0, 2),
+    ("v", 1, 0, 3),
+    ("v", 1, 1, 0),
+    ("v", 1, 2, 1),
+    ("r", 1, 2, 1),
+    ("v", 1, 1, 1),
+    ("r", 1, 2, 2),
+    ("r", 1, 2, 3),
+    ("v", 1, 2, 2),
+    ("v", 2, 1, 0),
+    ("v", 2, 2, 0),
+    ("v", 1, 2, 3),
+    ("v", 1, 1, 2),
+    ("v", 1, 1, 3),
+    ("v", 2, 0, 0),
+    ("v", 2, 2, 2),
+    ("gain", 0, 6),
+    ("v", 2, 1, 2),
+    ("v", 2, 0, 2),
+    ("gain", 0, 4),
+    ("gain", 1, 6),
+    ("gain", 1, 1),
+    ("gain", 1, 7),
+    ("gain", 1, 5),
+    ("gain", 1, 2),
+    ("gain", 1, 0),
+    ("gain", 2, 6),
+    ("gain", 2, 2),
+    ("gain", 1, 3),
+    ("gain", 1, 4),
+    ("gain", 2, 0),
+    ("plane", 0, 0),
+    ("gain", 2, 4),
+    ("plane", 0, 6),
+    ("plane", 0, 2),
+    ("plane", 0, 4),
+    ("plane", 1, 2),
+    ("plane", 1, 6),
+    ("plane", 1, 4),
+    ("plane", 1, 0),
+]
+RING = 4
+ITEM_COPY_ON_VECTOR = [1]
+CAST_V = [(0, 0), (0, 1), (0, 2), (0, 3), (0, 6), (0, 7), (1, 4), (2, 1), (2, 4), (2, 5)]
+
+
+def tile_facility_location_topic_gain_k4_kernel(
+    tc, cand_words, cand_scales, pool_words, pool_scales, cover, item_desc, topic_map, item_bias, cost, topic_scale,
+    out_0, out_1, out_2,
+):
+    nc = tc.nc
+    with ExitStack() as ctx:
+        keep = ctx.enter_context(tc.tile_pool(name="keep", bufs=1))
+        ring = ctx.enter_context(tc.tile_pool(name="ring", bufs=RING))
+        psum = ctx.enter_context(tc.psum_pool(name="psum", bufs=1))
+        ctx.enter_context(tc.manual_schedule(engines={mybir.EngineType.PE, mybir.EngineType.SP, mybir.EngineType.Pool}))
+
+        def kept(name, shape, dtype):
+            return keep.tile(shape, dtype, name=name, align_bytes=64)
+
+        banks_used = []
+
+        def next_bank(shape, dtype):
+            name = "bank%d" % (len(banks_used) % 8)
+            banks_used.append(name)
+            return psum.tile(shape, dtype, name=name)
+
+        a_codes = [kept("a_codes%d" % h, [P, EMB_PASSES, BANK], U32) for h in range(2)]
+        a_scales = kept("a_scales", [P, EMB_PASSES, CANDS], U8)
+        b_raw = [kept("b_raw%d" % g, [P, EMB_PASSES, 2 * KPASS], U8) for g in range(GROUPS)]
+        b_codes = [kept("b_codes%d" % g, [P, PACK, EMB_PASSES, 2 * P], U8) for g in range(GROUPS)]
+        b_scales_raw = kept("b_scales_raw", [P, EMB_PASSES, POOL], U8)
+        b_scales = kept("b_scales", [P, PACK, EMB_PASSES, GROUPS, P], U8)
+        items = [kept("items%d" % g, [P, PACK, DESC], BF16) for g in range(GROUPS)]
+        item_words = [kept("item_words%d" % g, [P, P, 2 * PACK], F32) for g in range(GROUPS)]
+        item_codes = [kept("item_codes%d" % g, [P, KPASS], U32) for g in range(GROUPS)]
+        item_scales = [kept("item_scales%d" % g, [P, KPASS], U8) for g in range(GROUPS)]
+        map_raw = [kept("map_raw%d" % c, [P, PACK, hi - lo], BF16) for c, (lo, hi) in enumerate(CHUNKS)]
+        map_codes = kept("map_codes", [P, TOPICS], U32)
+        map_scales = kept("map_scales", [P, TOPICS], U8)
+        r_codes = [kept("r_codes%d" % g, [P, CANDS], U32) for g in range(GROUPS)]
+        r_scales = [kept("r_scales%d" % g, [P, CANDS], U8) for g in range(GROUPS)]
+        v_codes = [kept("v_codes%d" % g, [P, TOPICS], U32) for g in range(GROUPS)]
+        v_scales = [kept("v_scales%d" % g, [P, TOPICS], U8) for g in range(GROUPS)]
+        vec_rows = kept("vec_rows", [P, GROUPS, P], BF16)
+        cover_rows = kept("cover_rows", [P, GROUPS, P], BF16)
+        vec_cols = kept("vec_cols", [P, GROUPS, 16], F32)
+        neg_cover = kept("neg_cover", [P, GROUPS, PACK], F32)
+        scale_rows = kept("scale_rows", [P, TOPICS], BF16)
+        ident = kept("ident", [P, P], F32)
+        ident_bf16 = kept("ident_bf16", [P, P], BF16)
+        shuffle = kept("shuffle", [P, P], F32)
+        y = kept("y", [P, CAND_TILES, TOPICS], F32)
+        y_pairs = kept("y_pairs", [P, CAND_TILES, 2, TOPICS // PACK, 2], BF16)
+        y_words = [kept("y_words%d" % g, [P, CANDS, 2], F32) for g in range(2)]
+        y_codes = [kept("y_codes%d" % g, [P, CANDS], U32) for g in range(2)]
+        y_scales = [kept("y_scales%d" % g, [P, CANDS], U8) for g in range(2)]
+
+        nc.vector.memset(b_scales_raw[:].bitcast(I32), 0)
+        nc.vector.memset(a_scales[:].bitcast(I32), 0)
+        nc.gpsimd.memset(cover_rows[:], 0.0)
+        make_identity(nc, ident[:])
+        nc.gpsimd.memset(vec_rows[:], 0.0)
+
+        cand_rows = cand_words.rearrange("g p n t -> p g (n t)")
+        pool_rows = pool_words.rearrange("g p n -> p g n")
+        map_rows = topic_map.rearrange("(p j) w -> p j w", j=PACK)
+
+        def load_planes(plane, scales):
+            rows = scales.rearrange("g q n -> q g n")
+            for quad in range(4):
+                nc.sync.dma_start(out=plane[32 * quad : 32 * quad + 4].bitcast(I32), in_=rows[4 * quad : 4 * quad + 4].bitcast(I32))
+
+        for what in LOADS:
+            if what == "bs":
+                load_planes(b_scales_raw, pool_scales)
+            elif what == "as":
+                load_planes(a_scales, cand_scales)
+            elif what == "cv":
+                nc.sync.dma_start(
+                    out=cover_rows[:].rearrange("p g (q r) -> p (g q) r", r=8)[8:12], in_=cover.rearrange("(m t r) -> t m r", t=PACK, r=8)
+                )
+            elif what == "bi":
+                nc.sync.dma_start(
+                    out=vec_rows[:].rearrange("p g (q r) -> p (g q) r", r=8)[12:16], in_=item_bias.rearrange("(m t r) -> t m r", t=PACK, r=8)
+                )
+            elif what == "co":
+                nc.sync.dma_start(out=vec_rows[16:24, 0, :], in_=cost.rearrange("(j p) -> j p", p=P))
+            elif what == "ts":
+                nc.sync.dma_start(out=scale_rows[:], in_=topic_scale.partition_broadcast(P))
+            elif what[0] == "t":
+                c = int(what[1])
+                nc.sync.dma_start(out=map_raw[c][:], in_=map_rows[:, :, CHUNKS[c][0] : CHUNKS[c][1]])
+            elif what.startswith("a"):
+                h = int(what[1])
+                nc.sync.dma_start(out=a_codes[h][:].bitcast(I32), in_=cand_rows[:, :, 4 * BANK * h : 4 * BANK * (h + 1)].bitcast(I32))
+            elif what.startswith("b"):
+                g = int(what[1])
+                nc.sync.dma_start(out=b_raw[g][:].bitcast(I32), in_=pool_rows[:, :, 2 * KPASS * g : 2 * KPASS * (g + 1)].bitcast(I32))
+            else:
+                g = int(what[1])
+                nc.sync.dma_start(out=items[g][:], in_=item_desc[KPASS * g : KPASS * (g + 1), :].rearrange("(p j) e -> p j e", j=PACK))
+
+        nc.scalar.copy(out=ident_bf16[:], in_=ident[:])
+        nc.scalar.copy(
+            out=shuffle[:].rearrange("p (t q h) -> p t q h", t=PACK, h=2),
+            in_=ident[:].rearrange("p (q t h) -> p t q h", t=PACK, h=2),
+        )
+
+        def interleave(dst, src):
+            nc.vector.tensor_copy(
+                out=dst.rearrange("p (c i) t -> p c t i", i=4), in_=src.rearrange("p t (c i) -> p c t i", i=4)
+            )
+
+        def quantise(codes, scales, values):
+            nc.vector.quantize_mx(out=codes.bitcast(FP8X4), scales=scales, in_=values)
+
+        def sort_b_scales():
+            def act():
+                nc.vector.tensor_copy(
+                    out=b_scales[:].rearrange("p t e g m -> p t (e g m)").bitcast(I32).rearrange("p t (m w) -> p t m w", w=2),
+                    in_=b_scales_raw[:].rearrange("p e n -> p (e n)").bitcast(I32).rearrange("p (m t w) -> p t m w", t=PACK, w=2),
+                )
+            return [(0, act)]
+
+        def sort_b_codes(g):
+            def act():
+                nc.vector.tensor_copy(
+                    out=b_codes[g][:].rearrange("p t e n -> p t (e n)").bitcast(I32).rearrange("p t (m w) -> p t m w", w=4),
+                    in_=b_raw[g][:].rearrange("p e n -> p (e n)").bitcast(I32).rearrange("p (m t w) -> p t m w", t=PACK, w=4),
+                )
+            return [(0, act)]
+
+        def vectors(which):
+            bank = next_bank([P, GROUPS, P], BF16)
+
+            def turn():
+                for g in range(GROUPS):
+                    nc.tensor.transpose(bank[:, g, :], (cover_rows, vec_rows)[which][:, g, :], ident_bf16[:])
+
+            def drain():
+                if which == 0:
+                    nc.scalar.activation(out=neg_cover[:], in_=bank[:, :, 8:12], func=ACT.Copy, scale=-1.0)
+                else:
+                    nc.scalar.copy(out=vec_cols[:], in_=bank[:, :, 8:24])
+            return [(0, turn), (1, drain)]
+
+        def item_bank(g, jp):
+            bank = next_bank([P, PACK, P], F32)
+            words = items[g][:].bitcast(F32)
+
+            def turn():
+                for j in range(2):
+                    for u in range(2):
+                        nc.tensor.transpose(bank[:, 2 * j + u, :], words[:, 2 * jp + j, u::2], shuffle[:])
+
+            def drain():
+                copy = nc.vector.tensor_copy if g in ITEM_COPY_ON_VECTOR else nc.scalar.copy
+                copy(out=item_words[g][:, :, PACK * jp : PACK * (jp + 1)], in_=bank[:].rearrange("p a n -> p n a"))
+
+            def quant():
+                quantise(item_codes[g][:], item_scales[g][:], item_words[g][:].rearrange("p n w -> p (n w)").bitcast(BF16))
+            return [(0, turn), (1, drain)] + ([(2, quant)] if jp == 1 else [])
+
+        def map_chunk(c):
+            lo, hi = CHUNKS[c]
+            src = map_raw[c][:]
+            mixed = ring.tile([P, hi - lo, PACK], BF16, name="mixed", align_bytes=64)
+            return [
+                (0, lambda: interleave(mixed[:], src)),
+                (1, lambda: quantise(map_codes[:, lo:hi], map_scales[:, lo:hi], mixed[:].rearrange("p n t -> p (n t)"))),
+            ]
+
+        def finish(rows, codes, scales, width):
+            mixed = ring.tile([P, width, PACK], BF16, name="mixed", align_bytes=64)
+            return [
+                (2, lambda: interleave(mixed[:], rows[:])),
+                (3, lambda: quantise(codes, scales, mixed[:].rearrange("p n t -> p (n t)"))),
+            ]
+
+        staged = {}
+        planes_done = []
+
+        def r_bank(h, g, t):
+            bank = next_bank([P, BANK], F32)
+            if t == 0:
+                staged["r", h, g] = ring.tile([P, PACK, BANK], BF16, name="rows", align_bytes=64)
+            rows = staged["r", h, g]
+            cols = slice(BANK * h, BANK * (h + 1))
+
+            def multiply():
+                for e in range(EMB_PASSES):
+                    nc.tensor.matmul_mx(
+                        out=bank[:], lhsT=b_codes[g][:, t, e, :].bitcast(FP4X4), lhsT_scale=b_scales[:, t, e, g, :],
+                        rhs=a_codes[h][:, e, :].bitcast(FP8X4), rhs_scale=a_scales[:, e, cols],
+                        start=(e == 0), stop=(e == EMB_PASSES - 1),
+                    )
+
+            def drain():
+                nc.scalar.activation(out=rows[:, t, :], in_=bank[:], func=ACT.Relu, bias=neg_cover[:, g, t : t + 1])
+            tail = finish(rows, r_codes[g][:, cols], r_scales[g][:, cols], BANK) if t == PACK - 1 else []
+            return [(0, multiply), (1, drain)] + tail
+
+        def v_bank(c, g, t0):
+            lo, hi = CHUNKS[c]
+            width = hi - lo
+            slots = range(t0, t0 + BANK // width)
+            bank = next_bank([P, len(slots), width], F32)
+            if t0 == 0:
+                staged["v", c, g] = ring.tile([P, PACK, width], BF16, name="rows", align_bytes=64)
+            rows = staged["v", c, g]
+
+            def multiply():
+                for t in slots:
+                    nc.tensor.matmul_mx(
+                        out=bank[:, t - t0, :], lhsT=item_codes[g][:, P * t : P * (t + 1)].bitcast(FP8X4),
+                        lhsT_scale=item_scales[g][:, P * t : P * (t + 1)],
+                        rhs=map_codes[:, lo:hi].bitcast(FP8X4), rhs_scale=map_scales[:, lo:hi], start=True, stop=True,
+                    )
+
+            def drain():
+                for t in slots:
+                    nc.scalar.activation(
+                        out=rows[:, t, :], in_=bank[:, t - t0, :], func=ACT.Identity, bias=vec_cols[:, g, PACK + t : PACK + t + 1]
+                    )
+            tail = finish(rows, v_codes[g][:, lo:hi], v_scales[g][:, lo:hi], width) if slots[-1] == PACK - 1 else []
+            return [(0, multiply), (1, drain)] + tail
+
+        def gain_bank(c, j0):
+            lo, hi = CHUNKS[c]
+            width = hi - lo
+            tiles = range(j0, j0 + BANK // width)
+            bank = next_bank([P, len(tiles), width], F32)
+
+            def multiply():
+                for j in tiles:
+                    for g in range(GROUPS):
+                        nc.tensor.matmul_mx(
+                            out=bank[:, j - j0, :], lhsT=r_codes[g][:, P * j : P * (j + 1)].bitcast(FP8X4),
+                            lhsT_scale=r_scales[g][:, P * j : P * (j + 1)],
+                            rhs=v_codes[g][:, lo:hi].bitcast(FP8X4), rhs_scale=v_scales[g][:, lo:hi],
+                            start=(g == 0), stop=(g == GROUPS - 1),
+                        )
+
+            def drain():
+                for j in tiles:
+                    nc.vector.scalar_tensor_tensor(
+                        out=y[:, j, lo:hi], in0=bank[:, j - j0, :], scalar=vec_cols[:, 0, 8 + j : 9 + j],
+                        in1=scale_rows[:, lo:hi], op0=ALU.subtract, op1=ALU.mult,
+                    )
+                nc.sync.dma_start(
+                    out=out_0[P * j0 : P * (tiles[-1] + 1), lo:hi].rearrange("(a p) n -> p a n", p=P),
+                    in_=y[:, j0 : tiles[-1] + 1, lo:hi],
+                )
+
+            def cast():
+                for j in tiles:
+                    src = y[:, j, lo:hi].rearrange("p (m u e) -> p u m e", u=2, e=2)
+                    dst = y_pairs[:, j, :, lo // PACK : hi // PACK, :]
+                    if (c, j) not in CAST_V if CAST_V is not None else CAST_ON_SCALAR[c]:
+                        nc.scalar.copy(out=dst, in_=src)
+                    else:
+                        nc.vector.tensor_copy(out=dst, in_=src)
+            return [(0, multiply), (1, drain), (2, cast)]
+
+        def plane_bank(g, j0):
+            bank = next_bank([P, 2, 2, P], F32)
+            words = y_pairs[:].rearrange("p j u m e -> p j u (m e)").bitcast(F32)
+            cols = slice(P * j0, P * (j0 + 2))
+
+            def turn():
+                for a in range(2):
+                    for u in range(2):
+                        nc.tensor.transpose(bank[:, u, a, :], words[:, j0 + a, u, P * g : P * (g + 1)], ident[:])
+
+            def drain():
+                nc.scalar.copy(out=y_words[g][:, cols, :], in_=bank[:].rearrange("p u a n -> p (a n) u"))
+
+            def quant():
+                quantise(y_codes[g][:, cols], y_scales[g][:, cols], y_words[g][:, cols, :].rearrange("p n u -> p (n u)").bitcast(BF16))
+                nc.sync.dma_start(
+                    out=out_1[g].rearrange("p m t -> p (m t)")[:, PACK * P * j0 : PACK * P * (j0 + 2)].bitcast(I32),
+                    in_=y_codes[g][:, cols].bitcast(I32),
+                )
+                planes_done.append(g)
+                if planes_done.count(g) == CAND_TILES // 2:
+                    for quad in range(4):
+                        nc.sync.dma_start(
+                            out=out_2[g, 4 * quad : 4 * quad + 4, :].bitcast(I32),
+                            in_=y_scales[g][32 * quad : 32 * quad + 4, :].bitcast(I32),
+                        )
+            return [(0, turn), (1, drain), (2, quant)]
+
+        makers = {"bs": sort_b_scales, "bc": sort_b_codes, "vec": vectors, "item": item_bank, "map": map_chunk,
+                  "r": r_bank, "v": v_bank, "gain": gain_bank, "plane": plane_bank, "nop": lambda: []}
+        order = ORDER if ORDER else schedule()
+        for unit in order:
+            for lag, act in makers[unit[0]](*unit[1:]):
+                act()
+
+
+def schedule():
+    def r_group(h, g):
+        return [("r", h, g, t) for t in range(PACK)]
+
+    def v_group(c, g):
+        lo, hi = CHUNKS[c]
+        return [("v", c, g, t) for t in range(0, PACK, BANK // (hi - lo))]
+
+    def weave(main, extra, every, offset=0):
+        woven = []
+        rest = list(extra)
+        for i, unit in enumerate(main):
+            woven.append(unit)
+            if i >= offset and (i - offset) % every == every - 1 and rest:
+                woven.append(rest[0])
+                rest = rest[1:]
+        return woven + rest
+
+    order = [("map", 0), ("vec", 0), ("item", 0, 0), ("item", 0, 1), ("bs",), ("vec", 1), ("bc", 0)]
+    order += v_group(0, 0) + [("item", 1, 0), ("item", 1, 1)] + r_group(0, 0) + [("bc", 1), ("map", 1)]
+    order += v_group(0, 1) + [("item", 2, 0), ("item", 2, 1)] + r_group(0, 1) + [("bc", 2)]
+    order += v_group(0, 2) + r_group(0, 2) + r_group(1, 0) + [("map", 2)]
+    order += weave(r_group(1, 1) + v_group(1, 0) + r_group(1, 2), [("gain", 0, 0), ("gain", 0, 2)], 4)
+    order += weave(v_group(1, 1) + v_group(1, 2) + v_group(2, 0), [("gain", 0, 4), ("gain", 0, 6)], 4, 2)
+    order += v_group(2, 1)
+    order += weave([("gain", 1, j) for j in range(8)], v_group(2, 2), 1)
+    order += [("plane", 0, 0), ("plane", 0, 2), ("gain", 2, 0), ("gain", 2, 2), ("plane", 0, 4), ("plane", 0, 6)]
+    order += [("gain", 2, 4), ("gain", 2, 6), ("plane", 1, 0), ("plane", 1, 2), ("plane", 1, 4), ("plane", 1, 6)]
+    return order

@@ -24,100 +24,102 @@ GROUPS = POOL // KPASS
 EMB_PASSES = EMB // KPASS
 CAND_TILES = CANDS // P
 CHUNKS = [(0, 256), (256, 768), (768, 1024)]
-LOADS = ["i0","b0","cv","t0","i1","bi","i2","b2","co","ts","bs","b1","a0","as","t2","t1","a1"]
+LOADS = ["i0","bs","i1","t0","as","co","b0","a0","b2","b1","t1","a1","i2","t2","ts"]
 CAST_ON_SCALAR = {0: False, 1: True, 2: False}
 ORDER = [
     ("item", 0, 0),
-    ("vec", 0),
-    ("bc", 1),
     ("item", 0, 1),
-    ("map", 0),
-    ("bs",),
-    ("item", 1, 0),
-    ("item", 1, 1),
-    ("bc", 0),
-    ("vec", 1),
-    ("v", 0, 0, 0),
-    ("v", 0, 0, 2),
-    ("item", 2, 0),
-    ("item", 2, 1),
-    ("r", 0, 0, 0),
     ("map", 1),
+    ("map", 0),
+    ("item", 1, 0),
+    ("bc", 0),
+    ("bs",),
+    ("item", 1, 1),
+    ("vec",),
+    ("cost",),
+    ("v", 0, 0, 0),
+    ("r", 0, 0, 0),
+    ("v", 0, 0, 2),
     ("v", 0, 1, 0),
+    ("v", 0, 1, 2),
+    ("bc", 1),
     ("map", 2),
     ("r", 0, 0, 1),
-    ("bc", 2),
-    ("v", 0, 1, 2),
-    ("r", 0, 0, 2),
-    ("v", 0, 2, 0),
     ("r", 0, 1, 0),
-    ("r", 0, 0, 3),
+    ("r", 0, 1, 1),
+    ("bc", 2),
+    ("r", 0, 0, 2),
     ("r", 0, 2, 0),
+    ("r", 0, 0, 3),
     ("r", 0, 2, 1),
+    ("r", 0, 1, 2),
+    ("item", 2, 0),
+    ("r", 0, 1, 3),
+    ("r", 1, 0, 0),
+    ("v", 1, 0, 0),
+    ("r", 1, 0, 1),
+    ("r", 0, 2, 2),
+    ("v", 1, 0, 1),
+    ("item", 2, 1),
+    ("r", 0, 2, 3),
+    ("r", 1, 0, 2),
+    ("v", 1, 1, 0),
+    ("r", 1, 0, 3),
+    ("v", 1, 1, 1),
+    ("v", 0, 2, 0),
+    ("v", 0, 2, 2),
+    ("v", 1, 0, 2),
+    ("v", 1, 0, 3),
+    ("v", 1, 1, 2),
+    ("v", 1, 2, 0),
+    ("v", 1, 2, 1),
+    ("v", 1, 2, 2),
+    ("v", 1, 1, 3),
+    ("v", 1, 2, 3),
+    ("gain", 0, 0),
     ("r", 1, 1, 0),
     ("r", 1, 1, 1),
-    ("r", 0, 2, 2),
-    ("r", 0, 2, 3),
-    ("v", 0, 2, 2),
-    ("r", 0, 1, 1),
-    ("r", 0, 1, 2),
-    ("r", 0, 1, 3),
-    ("r", 1, 1, 2),
-    ("r", 1, 0, 0),
-    ("r", 1, 0, 1),
     ("r", 1, 2, 0),
+    ("r", 1, 1, 2),
     ("r", 1, 1, 3),
-    ("r", 1, 0, 2),
-    ("v", 1, 2, 0),
-    ("v", 1, 0, 0),
-    ("r", 1, 0, 3),
-    ("v", 1, 0, 1),
-    ("v", 1, 0, 2),
-    ("gain", 0, 0),
-    ("gain", 0, 2),
-    ("v", 1, 0, 3),
-    ("v", 1, 1, 0),
-    ("v", 1, 2, 1),
     ("r", 1, 2, 1),
-    ("v", 1, 1, 1),
     ("r", 1, 2, 2),
+    ("gain", 1, 3),
     ("r", 1, 2, 3),
-    ("v", 1, 2, 2),
-    ("v", 2, 1, 0),
-    ("v", 2, 2, 0),
-    ("v", 1, 2, 3),
-    ("v", 1, 1, 2),
-    ("v", 1, 1, 3),
-    ("v", 2, 0, 0),
-    ("v", 2, 2, 2),
-    ("gain", 0, 6),
-    ("v", 2, 1, 2),
-    ("v", 2, 0, 2),
-    ("gain", 0, 4),
-    ("gain", 1, 6),
     ("gain", 1, 1),
-    ("gain", 1, 7),
-    ("gain", 1, 5),
+    ("v", 2, 0, 0),
+    ("v", 2, 0, 2),
+    ("v", 2, 2, 0),
+    ("v", 2, 2, 2),
+    ("v", 2, 1, 0),
+    ("v", 2, 1, 2),
     ("gain", 1, 2),
     ("gain", 1, 0),
-    ("gain", 2, 6),
-    ("gain", 2, 2),
-    ("gain", 1, 3),
+    ("gain", 1, 5),
+    ("gain", 1, 6),
+    ("gain", 0, 2),
     ("gain", 1, 4),
-    ("gain", 2, 0),
-    ("plane", 0, 0),
+    ("gain", 0, 4),
+    ("gain", 2, 2),
     ("gain", 2, 4),
-    ("plane", 0, 6),
-    ("plane", 0, 2),
-    ("plane", 0, 4),
-    ("plane", 1, 2),
-    ("plane", 1, 6),
-    ("plane", 1, 4),
-    ("plane", 1, 0),
+    ("gain", 1, 7),
+    ("gain", 0, 6),
+    ("gain", 2, 6),
+    ("gain", 2, 0),
+    ("plane", 1, 2, 2),
+    ("plane", 0, 6, 2),
+    ("plane", 0, 4, 2),
+    ("plane", 1, 5, 1),
+    ("plane", 1, 4, 1),
+    ("plane", 1, 6, 2),
+    ("plane", 1, 0, 2),
+    ("plane", 0, 2, 2),
+    ("plane", 0, 0, 2),
 ]
 RING = 4
-ITEM_COPY_ON_VECTOR = [1]
-CAST_V = [(0, 0), (0, 1), (0, 2), (0, 3), (0, 6), (0, 7), (1, 4), (2, 1), (2, 4), (2, 5)]
+ITEM_COPY_ON_VECTOR = [0,2]
+CAST_V = [(0, 0), (2, 0), (2, 1), (9, 1, 2), (9, 1, 4), (9, 1, 5)]
+PLANE_V = [(1, 2), (1, 4), (1, 5)]
 
 
 def tile_facility_location_topic_gain_k4_kernel(
@@ -158,10 +160,12 @@ def tile_facility_location_topic_gain_k4_kernel(
         r_scales = [kept("r_scales%d" % g, [P, CANDS], U8) for g in range(GROUPS)]
         v_codes = [kept("v_codes%d" % g, [P, TOPICS], U32) for g in range(GROUPS)]
         v_scales = [kept("v_scales%d" % g, [P, TOPICS], U8) for g in range(GROUPS)]
-        vec_rows = kept("vec_rows", [P, GROUPS, P], BF16)
-        cover_rows = kept("cover_rows", [P, GROUPS, P], BF16)
-        vec_cols = kept("vec_cols", [P, GROUPS, 16], F32)
-        neg_cover = kept("neg_cover", [P, GROUPS, PACK], F32)
+        vec_raw = kept("vec_raw", [P, KPASS], BF16)
+        vec_rows = kept("vec_rows", [P, PACK, P], BF16)
+        vec_cols = kept("vec_cols", [P, PACK, GROUPS], F32)
+        cost_rows = kept("cost_rows", [P, P], BF16)
+        cost_cols = kept("cost_cols", [P, CAND_TILES], F32)
+        neg_cover = kept("neg_cover", [P, PACK, GROUPS], F32)
         scale_rows = kept("scale_rows", [P, TOPICS], BF16)
         ident = kept("ident", [P, P], F32)
         ident_bf16 = kept("ident_bf16", [P, P], BF16)
@@ -170,13 +174,15 @@ def tile_facility_location_topic_gain_k4_kernel(
         y_pairs = kept("y_pairs", [P, CAND_TILES, 2, TOPICS // PACK, 2], BF16)
         y_words = [kept("y_words%d" % g, [P, CANDS, 2], F32) for g in range(2)]
         y_codes = [kept("y_codes%d" % g, [P, CANDS], U32) for g in range(2)]
-        y_scales = [kept("y_scales%d" % g, [P, CANDS], U8) for g in range(2)]
+        y_scales = kept("y_scales", [P, 2, CANDS], U8)
 
         nc.vector.memset(b_scales_raw[:].bitcast(I32), 0)
         nc.vector.memset(a_scales[:].bitcast(I32), 0)
-        nc.gpsimd.memset(cover_rows[:], 0.0)
-        make_identity(nc, ident[:])
+        nc.scalar.dma_start(out=vec_raw[0:GROUPS, :], in_=cover.rearrange("(g n) -> g n", g=GROUPS))
+        nc.scalar.dma_start(out=vec_raw[GROUPS : 2 * GROUPS, :], in_=item_bias.rearrange("(g n) -> g n", g=GROUPS))
         nc.gpsimd.memset(vec_rows[:], 0.0)
+        make_identity(nc, ident[:])
+        nc.gpsimd.memset(cost_rows[:], 0.0)
 
         cand_rows = cand_words.rearrange("g p n t -> p g (n t)")
         pool_rows = pool_words.rearrange("g p n -> p g n")
@@ -185,23 +191,15 @@ def tile_facility_location_topic_gain_k4_kernel(
         def load_planes(plane, scales):
             rows = scales.rearrange("g q n -> q g n")
             for quad in range(4):
-                nc.sync.dma_start(out=plane[32 * quad : 32 * quad + 4].bitcast(I32), in_=rows[4 * quad : 4 * quad + 4].bitcast(I32))
+                nc.sync.dma_start(out=plane[quad:P:32].bitcast(I32), in_=rows[quad:16:4].bitcast(I32))
 
         for what in LOADS:
             if what == "bs":
                 load_planes(b_scales_raw, pool_scales)
             elif what == "as":
                 load_planes(a_scales, cand_scales)
-            elif what == "cv":
-                nc.sync.dma_start(
-                    out=cover_rows[:].rearrange("p g (q r) -> p (g q) r", r=8)[8:12], in_=cover.rearrange("(m t r) -> t m r", t=PACK, r=8)
-                )
-            elif what == "bi":
-                nc.sync.dma_start(
-                    out=vec_rows[:].rearrange("p g (q r) -> p (g q) r", r=8)[12:16], in_=item_bias.rearrange("(m t r) -> t m r", t=PACK, r=8)
-                )
             elif what == "co":
-                nc.sync.dma_start(out=vec_rows[16:24, 0, :], in_=cost.rearrange("(j p) -> j p", p=P))
+                nc.sync.dma_start(out=cost_rows[0:CAND_TILES, :], in_=cost.rearrange("(j p) -> j p", p=P))
             elif what == "ts":
                 nc.sync.dma_start(out=scale_rows[:], in_=topic_scale.partition_broadcast(P))
             elif what[0] == "t":
@@ -247,19 +245,28 @@ def tile_facility_location_topic_gain_k4_kernel(
                 )
             return [(0, act)]
 
-        def vectors(which):
-            bank = next_bank([P, GROUPS, P], BF16)
+        def vectors():
+            bank = next_bank([P, PACK, P], BF16)
 
             def turn():
-                for g in range(GROUPS):
-                    nc.tensor.transpose(bank[:, g, :], (cover_rows, vec_rows)[which][:, g, :], ident_bf16[:])
+                nc.vector.tensor_copy(
+                    out=vec_rows[0 : 2 * GROUPS].rearrange("p t (q r) -> p t q r", r=8),
+                    in_=vec_raw[0 : 2 * GROUPS].rearrange("p (q t r) -> p t q r", t=PACK, r=8),
+                )
+                for t in range(PACK):
+                    nc.tensor.transpose(bank[:, t, :], vec_rows[:, t, :], ident_bf16[:])
 
             def drain():
-                if which == 0:
-                    nc.scalar.activation(out=neg_cover[:], in_=bank[:, :, 8:12], func=ACT.Copy, scale=-1.0)
-                else:
-                    nc.scalar.copy(out=vec_cols[:], in_=bank[:, :, 8:24])
+                nc.scalar.activation(out=neg_cover[:], in_=bank[:, :, 0:GROUPS], func=ACT.Copy, scale=-1.0)
+                nc.scalar.copy(out=vec_cols[:], in_=bank[:, :, GROUPS : 2 * GROUPS])
             return [(0, turn), (1, drain)]
+
+        def costs():
+            bank = next_bank([P, P], BF16)
+            return [
+                (0, lambda: nc.tensor.transpose(bank[:], cost_rows[:], ident_bf16[:])),
+                (1, lambda: nc.scalar.copy(out=cost_cols[:], in_=bank[:, 0:CAND_TILES])),
+            ]
 
         def item_bank(g, jp):
             bank = next_bank([P, PACK, P], F32)
@@ -313,7 +320,7 @@ def tile_facility_location_topic_gain_k4_kernel(
                     )
 
             def drain():
-                nc.scalar.activation(out=rows[:, t, :], in_=bank[:], func=ACT.Relu, bias=neg_cover[:, g, t : t + 1])
+                nc.scalar.activation(out=rows[:, t, :], in_=bank[:], func=ACT.Relu, bias=neg_cover[:, t, g : g + 1])
             tail = finish(rows, r_codes[g][:, cols], r_scales[g][:, cols], BANK) if t == PACK - 1 else []
             return [(0, multiply), (1, drain)] + tail
 
@@ -337,7 +344,7 @@ def tile_facility_location_topic_gain_k4_kernel(
             def drain():
                 for t in slots:
                     nc.scalar.activation(
-                        out=rows[:, t, :], in_=bank[:, t - t0, :], func=ACT.Identity, bias=vec_cols[:, g, PACK + t : PACK + t + 1]
+                        out=rows[:, t, :], in_=bank[:, t - t0, :], func=ACT.Identity, bias=vec_cols[:, t, g : g + 1]
                     )
             tail = finish(rows, v_codes[g][:, lo:hi], v_scales[g][:, lo:hi], width) if slots[-1] == PACK - 1 else []
             return [(0, multiply), (1, drain)] + tail
@@ -361,7 +368,7 @@ def tile_facility_location_topic_gain_k4_kernel(
             def drain():
                 for j in tiles:
                     nc.vector.scalar_tensor_tensor(
-                        out=y[:, j, lo:hi], in0=bank[:, j - j0, :], scalar=vec_cols[:, 0, 8 + j : 9 + j],
+                        out=y[:, j, lo:hi], in0=bank[:, j - j0, :], scalar=cost_cols[:, j : j + 1],
                         in1=scale_rows[:, lo:hi], op0=ALU.subtract, op1=ALU.mult,
                     )
                 nc.sync.dma_start(
@@ -379,35 +386,37 @@ def tile_facility_location_topic_gain_k4_kernel(
                         nc.vector.tensor_copy(out=dst, in_=src)
             return [(0, multiply), (1, drain), (2, cast)]
 
-        def plane_bank(g, j0):
-            bank = next_bank([P, 2, 2, P], F32)
+        def plane_bank(g, j0, count):
+            bank = next_bank([P, 2, count, P], F32)
             words = y_pairs[:].rearrange("p j u m e -> p j u (m e)").bitcast(F32)
-            cols = slice(P * j0, P * (j0 + 2))
+            cols = slice(P * j0, P * (j0 + count))
 
             def turn():
-                for a in range(2):
+                for a in range(count):
                     for u in range(2):
                         nc.tensor.transpose(bank[:, u, a, :], words[:, j0 + a, u, P * g : P * (g + 1)], ident[:])
 
             def drain():
-                nc.scalar.copy(out=y_words[g][:, cols, :], in_=bank[:].rearrange("p u a n -> p (a n) u"))
+                copy = nc.vector.tensor_copy if (g, j0) in PLANE_V else nc.scalar.copy
+                copy(out=y_words[g][:, cols, :], in_=bank[:].rearrange("p u a n -> p (a n) u"))
 
             def quant():
-                quantise(y_codes[g][:, cols], y_scales[g][:, cols], y_words[g][:, cols, :].rearrange("p n u -> p (n u)").bitcast(BF16))
-                nc.sync.dma_start(
-                    out=out_1[g].rearrange("p m t -> p (m t)")[:, PACK * P * j0 : PACK * P * (j0 + 2)].bitcast(I32),
-                    in_=y_codes[g][:, cols].bitcast(I32),
-                )
-                planes_done.append(g)
-                if planes_done.count(g) == CAND_TILES // 2:
+                quantise(y_codes[g][:, cols], y_scales[:, g, cols], y_words[g][:, cols, :].rearrange("p n u -> p (n u)").bitcast(BF16))
+                half = j0 // 4
+                planes_done.extend([(g, half)] * count)
+                if planes_done.count((g, half)) == 4:
+                    nc.sync.dma_start(
+                        out=out_1[g].rearrange("p m t -> p (m t)")[:, PACK * BANK * half : PACK * BANK * (half + 1)].bitcast(I32),
+                        in_=y_codes[g][:, BANK * half : BANK * (half + 1)].bitcast(I32),
+                    )
+                if len(planes_done) == 2 * CAND_TILES:
                     for quad in range(4):
                         nc.sync.dma_start(
-                            out=out_2[g, 4 * quad : 4 * quad + 4, :].bitcast(I32),
-                            in_=y_scales[g][32 * quad : 32 * quad + 4, :].bitcast(I32),
+                            out=out_2.rearrange("g q m -> q g m")[quad:16:4].bitcast(I32), in_=y_scales[quad:P:32].bitcast(I32)
                         )
             return [(0, turn), (1, drain), (2, quant)]
 
-        makers = {"bs": sort_b_scales, "bc": sort_b_codes, "vec": vectors, "item": item_bank, "map": map_chunk,
+        makers = {"bs": sort_b_scales, "bc": sort_b_codes, "vec": vectors, "cost": costs, "item": item_bank, "map": map_chunk,
                   "r": r_bank, "v": v_bank, "gain": gain_bank, "plane": plane_bank, "nop": lambda: []}
         order = ORDER if ORDER else schedule()
         for unit in order:
@@ -433,7 +442,7 @@ def schedule():
                 rest = rest[1:]
         return woven + rest
 
-    order = [("map", 0), ("vec", 0), ("item", 0, 0), ("item", 0, 1), ("bs",), ("vec", 1), ("bc", 0)]
+    order = [("map", 0), ("vec",), ("cost",), ("item", 0, 0), ("item", 0, 1), ("bs",), ("bc", 0)]
     order += v_group(0, 0) + [("item", 1, 0), ("item", 1, 1)] + r_group(0, 0) + [("bc", 1), ("map", 1)]
     order += v_group(0, 1) + [("item", 2, 0), ("item", 2, 1)] + r_group(0, 1) + [("bc", 2)]
     order += v_group(0, 2) + r_group(0, 2) + r_group(1, 0) + [("map", 2)]
@@ -441,6 +450,6 @@ def schedule():
     order += weave(v_group(1, 1) + v_group(1, 2) + v_group(2, 0), [("gain", 0, 4), ("gain", 0, 6)], 4, 2)
     order += v_group(2, 1)
     order += weave([("gain", 1, j) for j in range(8)], v_group(2, 2), 1)
-    order += [("plane", 0, 0), ("plane", 0, 2), ("gain", 2, 0), ("gain", 2, 2), ("plane", 0, 4), ("plane", 0, 6)]
-    order += [("gain", 2, 4), ("gain", 2, 6), ("plane", 1, 0), ("plane", 1, 2), ("plane", 1, 4), ("plane", 1, 6)]
+    order += [("plane", 0, 0, 2), ("plane", 0, 2, 2), ("gain", 2, 0), ("gain", 2, 2), ("plane", 0, 4, 2), ("plane", 0, 6, 2)]
+    order += [("gain", 2, 4), ("gain", 2, 6), ("plane", 1, 0, 2), ("plane", 1, 2, 2), ("plane", 1, 4, 2), ("plane", 1, 6, 2)]
     return order

@@ -23,103 +23,108 @@ BANK = 512
 GROUPS = POOL // KPASS
 EMB_PASSES = EMB // KPASS
 CAND_TILES = CANDS // P
-CHUNKS = [(0, 256), (256, 768), (768, 1024)]
-LOADS = ["i0","bs","i1","t0","as","co","b0","a0","b2","b1","t1","a1","i2","t2","ts"]
+CHUNKS = [(0, 512), (512, 1024)]
+LOADS = ["i0","t0","i1","bs","t1","b0","i2","as","a0","b1","b2","a1","co","ts"]
 CAST_ON_SCALAR = {0: False, 1: True, 2: False}
 ORDER = [
     ("item", 0, 0),
     ("item", 0, 1),
-    ("map", 1),
-    ("map", 0),
-    ("item", 1, 0),
-    ("bc", 0),
-    ("bs",),
-    ("item", 1, 1),
     ("vec",),
-    ("cost",),
+    ("item", 1, 0),
+    ("item", 1, 1),
+    ("map", 0),
+    ("nop",),
+    ("nop",),
+    ("nop",),
+    ("nop",),
     ("v", 0, 0, 0),
-    ("r", 0, 0, 0),
+    ("v", 0, 0, 1),
     ("v", 0, 0, 2),
+    ("v", 0, 0, 3),
+    ("map", 1),
+    ("bs",),
     ("v", 0, 1, 0),
+    ("v", 0, 1, 1),
     ("v", 0, 1, 2),
-    ("bc", 1),
-    ("map", 2),
-    ("r", 0, 0, 1),
-    ("r", 0, 1, 0),
-    ("r", 0, 1, 1),
-    ("bc", 2),
-    ("r", 0, 0, 2),
-    ("r", 0, 2, 0),
-    ("r", 0, 0, 3),
-    ("r", 0, 2, 1),
-    ("r", 0, 1, 2),
+    ("v", 0, 1, 3),
+    ("bc", 0),
     ("item", 2, 0),
-    ("r", 0, 1, 3),
-    ("r", 1, 0, 0),
-    ("v", 1, 0, 0),
-    ("r", 1, 0, 1),
-    ("r", 0, 2, 2),
-    ("v", 1, 0, 1),
     ("item", 2, 1),
-    ("r", 0, 2, 3),
-    ("r", 1, 0, 2),
-    ("v", 1, 1, 0),
-    ("r", 1, 0, 3),
-    ("v", 1, 1, 1),
-    ("v", 0, 2, 0),
-    ("v", 0, 2, 2),
+    ("v", 1, 0, 0),
+    ("v", 1, 0, 1),
     ("v", 1, 0, 2),
     ("v", 1, 0, 3),
+    ("bc", 1),
+    ("r", 0, 0, 0),
+    ("r", 0, 0, 1),
+    ("r", 0, 0, 2),
+    ("r", 0, 0, 3),
+    ("bc", 2),
+    ("r", 0, 1, 0),
+    ("v", 0, 2, 0),
+    ("r", 0, 1, 1),
+    ("v", 0, 2, 1),
+    ("r", 0, 1, 2),
+    ("v", 0, 2, 2),
+    ("r", 0, 1, 3),
+    ("v", 0, 2, 3),
+    ("r", 0, 2, 0),
+    ("r", 0, 2, 1),
+    ("r", 0, 2, 2),
+    ("r", 0, 2, 3),
+    ("r", 1, 0, 0),
+    ("r", 1, 0, 1),
+    ("r", 1, 0, 2),
+    ("r", 1, 0, 3),
+    ("r", 1, 1, 0),
+    ("r", 1, 1, 1),
+    ("r", 1, 1, 2),
+    ("r", 1, 1, 3),
+    ("r", 1, 2, 0),
+    ("r", 1, 2, 1),
+    ("r", 1, 2, 2),
+    ("r", 1, 2, 3),
+    ("cost",),
+    ("v", 1, 1, 0),
+    ("v", 1, 1, 1),
+    ("gain", 0, 0),
     ("v", 1, 1, 2),
+    ("v", 1, 1, 3),
     ("v", 1, 2, 0),
     ("v", 1, 2, 1),
     ("v", 1, 2, 2),
-    ("v", 1, 1, 3),
     ("v", 1, 2, 3),
-    ("gain", 0, 0),
-    ("r", 1, 1, 0),
-    ("r", 1, 1, 1),
-    ("r", 1, 2, 0),
-    ("r", 1, 1, 2),
-    ("r", 1, 1, 3),
-    ("r", 1, 2, 1),
-    ("r", 1, 2, 2),
-    ("gain", 1, 3),
-    ("r", 1, 2, 3),
-    ("gain", 1, 1),
-    ("v", 2, 0, 0),
-    ("v", 2, 0, 2),
-    ("v", 2, 2, 0),
-    ("v", 2, 2, 2),
-    ("v", 2, 1, 0),
-    ("v", 2, 1, 2),
-    ("gain", 1, 2),
+    ("gain", 0, 1),
+    ("gain", 0, 2),
+    ("gain", 0, 3),
+    ("gain", 0, 4),
+    ("gain", 0, 5),
+    ("gain", 0, 6),
+    ("gain", 0, 7),
+    ("plane", 0, 0, 2),
+    ("plane", 0, 2, 2),
     ("gain", 1, 0),
+    ("gain", 1, 1),
+    ("gain", 1, 2),
+    ("gain", 1, 3),
+    ("plane", 0, 4, 2),
+    ("plane", 0, 6, 2),
+    ("gain", 1, 4),
     ("gain", 1, 5),
     ("gain", 1, 6),
-    ("gain", 0, 2),
-    ("gain", 1, 4),
-    ("gain", 0, 4),
-    ("gain", 2, 2),
-    ("gain", 2, 4),
     ("gain", 1, 7),
-    ("gain", 0, 6),
-    ("gain", 2, 6),
-    ("gain", 2, 0),
-    ("plane", 1, 2, 2),
-    ("plane", 0, 6, 2),
-    ("plane", 0, 4, 2),
-    ("plane", 1, 5, 1),
-    ("plane", 1, 4, 1),
-    ("plane", 1, 6, 2),
     ("plane", 1, 0, 2),
-    ("plane", 0, 2, 2),
-    ("plane", 0, 0, 2),
+    ("plane", 1, 2, 2),
+    ("nop",),
+    ("plane", 1, 4, 2),
+    ("plane", 1, 6, 1),
+    ("plane", 1, 7, 1),
 ]
-RING = 4
-ITEM_COPY_ON_VECTOR = [0,2]
-CAST_V = [(0, 0), (2, 0), (2, 1), (9, 1, 2), (9, 1, 4), (9, 1, 5)]
-PLANE_V = [(1, 2), (1, 4), (1, 5)]
+RING = 5
+ITEM_COPY_ON_VECTOR = [2]
+CAST_V = [(1, 1), (1, 4), (1, 6), (1, 7), (9, 1, 6)]
+PLANE_V = [(1, 6)]
+LAG = {"drain":3,"mix":7,"quant":9,"cast":6,"plane":5,"item":9,"map":4}
 
 
 def tile_facility_location_topic_gain_k4_kernel(
@@ -131,7 +136,7 @@ def tile_facility_location_topic_gain_k4_kernel(
         keep = ctx.enter_context(tc.tile_pool(name="keep", bufs=1))
         ring = ctx.enter_context(tc.tile_pool(name="ring", bufs=RING))
         psum = ctx.enter_context(tc.psum_pool(name="psum", bufs=1))
-        ctx.enter_context(tc.manual_schedule(engines={mybir.EngineType.PE, mybir.EngineType.SP, mybir.EngineType.Pool}))
+        ctx.enter_context(tc.manual_schedule())
 
         def kept(name, shape, dtype):
             return keep.tile(shape, dtype, name=name, align_bytes=64)
@@ -180,10 +185,14 @@ def tile_facility_location_topic_gain_k4_kernel(
         nc.vector.memset(a_scales[:].bitcast(I32), 0)
         nc.scalar.dma_start(out=vec_raw[0:GROUPS, :], in_=cover.rearrange("(g n) -> g n", g=GROUPS))
         nc.scalar.dma_start(out=vec_raw[GROUPS : 2 * GROUPS, :], in_=item_bias.rearrange("(g n) -> g n", g=GROUPS))
-        nc.gpsimd.memset(vec_rows[:], 0.0)
         make_identity(nc, ident[:])
+        nc.gpsimd.memset(vec_rows[:], 0.0)
         nc.gpsimd.memset(cost_rows[:], 0.0)
 
+        nc.vector.tensor_copy(
+            out=shuffle[:].rearrange("p (t q h) -> p t q h", t=PACK, h=2),
+            in_=ident[:].rearrange("p (q t h) -> p t q h", t=PACK, h=2),
+        )
         cand_rows = cand_words.rearrange("g p n t -> p g (n t)")
         pool_rows = pool_words.rearrange("g p n -> p g n")
         map_rows = topic_map.rearrange("(p j) w -> p j w", j=PACK)
@@ -215,11 +224,7 @@ def tile_facility_location_topic_gain_k4_kernel(
                 g = int(what[1])
                 nc.sync.dma_start(out=items[g][:], in_=item_desc[KPASS * g : KPASS * (g + 1), :].rearrange("(p j) e -> p j e", j=PACK))
 
-        nc.scalar.copy(out=ident_bf16[:], in_=ident[:])
-        nc.scalar.copy(
-            out=shuffle[:].rearrange("p (t q h) -> p t q h", t=PACK, h=2),
-            in_=ident[:].rearrange("p (q t h) -> p t q h", t=PACK, h=2),
-        )
+        nc.scalar.activation(out=ident_bf16[:], in_=ident[:], func=ACT.Relu)
 
         def interleave(dst, src):
             nc.vector.tensor_copy(
@@ -283,23 +288,22 @@ def tile_facility_location_topic_gain_k4_kernel(
 
             def quant():
                 quantise(item_codes[g][:], item_scales[g][:], item_words[g][:].rearrange("p n w -> p (n w)").bitcast(BF16))
-            return [(0, turn), (1, drain)] + ([(2, quant)] if jp == 1 else [])
+            return [(0, turn), (LAG["drain"], drain)] + ([(LAG["item"], quant)] if jp == 1 else [])
+
+        def mix_and_quantise(src, codes, scales, width, mix_lag, quant_lag):
+            mixed = []
+
+            def mix():
+                mixed.append(ring.tile([P, width, PACK], BF16, name="mixed", align_bytes=64))
+                interleave(mixed[0][:], src())
+            return [(mix_lag, mix), (quant_lag, lambda: quantise(codes, scales, mixed[0][:].rearrange("p n t -> p (n t)")))]
 
         def map_chunk(c):
             lo, hi = CHUNKS[c]
-            src = map_raw[c][:]
-            mixed = ring.tile([P, hi - lo, PACK], BF16, name="mixed", align_bytes=64)
-            return [
-                (0, lambda: interleave(mixed[:], src)),
-                (1, lambda: quantise(map_codes[:, lo:hi], map_scales[:, lo:hi], mixed[:].rearrange("p n t -> p (n t)"))),
-            ]
+            return mix_and_quantise(lambda: map_raw[c][:], map_codes[:, lo:hi], map_scales[:, lo:hi], hi - lo, 0, LAG["map"])
 
         def finish(rows, codes, scales, width):
-            mixed = ring.tile([P, width, PACK], BF16, name="mixed", align_bytes=64)
-            return [
-                (2, lambda: interleave(mixed[:], rows[:])),
-                (3, lambda: quantise(codes, scales, mixed[:].rearrange("p n t -> p (n t)"))),
-            ]
+            return mix_and_quantise(lambda: rows[:], codes, scales, width, LAG["mix"], LAG["quant"])
 
         staged = {}
         planes_done = []
@@ -322,7 +326,7 @@ def tile_facility_location_topic_gain_k4_kernel(
             def drain():
                 nc.scalar.activation(out=rows[:, t, :], in_=bank[:], func=ACT.Relu, bias=neg_cover[:, t, g : g + 1])
             tail = finish(rows, r_codes[g][:, cols], r_scales[g][:, cols], BANK) if t == PACK - 1 else []
-            return [(0, multiply), (1, drain)] + tail
+            return [(0, multiply), (LAG["drain"], drain)] + tail
 
         def v_bank(c, g, t0):
             lo, hi = CHUNKS[c]
@@ -347,7 +351,7 @@ def tile_facility_location_topic_gain_k4_kernel(
                         out=rows[:, t, :], in_=bank[:, t - t0, :], func=ACT.Identity, bias=vec_cols[:, t, g : g + 1]
                     )
             tail = finish(rows, v_codes[g][:, lo:hi], v_scales[g][:, lo:hi], width) if slots[-1] == PACK - 1 else []
-            return [(0, multiply), (1, drain)] + tail
+            return [(0, multiply), (LAG["drain"], drain)] + tail
 
         def gain_bank(c, j0):
             lo, hi = CHUNKS[c]
@@ -384,7 +388,7 @@ def tile_facility_location_topic_gain_k4_kernel(
                         nc.scalar.copy(out=dst, in_=src)
                     else:
                         nc.vector.tensor_copy(out=dst, in_=src)
-            return [(0, multiply), (1, drain), (2, cast)]
+            return [(0, multiply), (LAG["drain"], drain), (LAG["cast"], cast)]
 
         def plane_bank(g, j0, count):
             bank = next_bank([P, 2, count, P], F32)
@@ -404,24 +408,26 @@ def tile_facility_location_topic_gain_k4_kernel(
                 quantise(y_codes[g][:, cols], y_scales[:, g, cols], y_words[g][:, cols, :].rearrange("p n u -> p (n u)").bitcast(BF16))
                 half = j0 // 4
                 planes_done.extend([(g, half)] * count)
-                if planes_done.count((g, half)) == 4:
-                    nc.sync.dma_start(
-                        out=out_1[g].rearrange("p m t -> p (m t)")[:, PACK * BANK * half : PACK * BANK * (half + 1)].bitcast(I32),
-                        in_=y_codes[g][:, BANK * half : BANK * (half + 1)].bitcast(I32),
-                    )
-                if len(planes_done) == 2 * CAND_TILES:
+                if planes_done.count((g, 0)) + planes_done.count((g, 1)) == CAND_TILES:
                     for quad in range(4):
-                        nc.sync.dma_start(
-                            out=out_2.rearrange("g q m -> q g m")[quad:16:4].bitcast(I32), in_=y_scales[quad:P:32].bitcast(I32)
-                        )
-            return [(0, turn), (1, drain), (2, quant)]
+                        nc.sync.dma_start(out=out_2[g, quad:16:4, :].bitcast(I32), in_=y_scales[quad:P:32, g, :].bitcast(I32))
+                if g == 1 or planes_done.count((g, half)) == 4:
+                    span = cols if g == 1 else slice(BANK * half, BANK * (half + 1))
+                    nc.sync.dma_start(
+                        out=out_1[g].rearrange("p m t -> p (m t)")[:, PACK * span.start : PACK * span.stop].bitcast(I32),
+                        in_=y_codes[g][:, span].bitcast(I32),
+                    )
+            return [(0, turn), (LAG["drain"], drain), (LAG["plane"], quant)]
 
         makers = {"bs": sort_b_scales, "bc": sort_b_codes, "vec": vectors, "cost": costs, "item": item_bank, "map": map_chunk,
                   "r": r_bank, "v": v_bank, "gain": gain_bank, "plane": plane_bank, "nop": lambda: []}
         order = ORDER if ORDER else schedule()
-        for unit in order:
-            for lag, act in makers[unit[0]](*unit[1:]):
-                act()
+        pending = []
+        for step in range(len(order) + max(LAG.values())):
+            if step < len(order):
+                pending.extend((step + lag, -lag, act) for lag, act in makers[order[step][0]](*order[step][1:]))
+            for due in sorted([e for e in pending if e[0] == step], key=lambda e: e[1]):
+                due[2]()
 
 
 def schedule():

@@ -17,114 +17,29 @@ CANDS, EMB, POOL, DESC, TOPICS = 1024, 1024, 1536, 512, 1024
 FLOPS = 2 * CANDS * POOL * EMB + 2 * POOL * TOPICS * DESC + 2 * CANDS * TOPICS * POOL
 
 P = 128
-PACK = 4
-KPASS = P * PACK
-BANK = 512
-GROUPS = POOL // KPASS
-EMB_PASSES = EMB // KPASS
+SLOTS = 4
+GROUP = P * SLOTS
+HALF = 512
+RUN = 8
+BANKS = 8
+POOL_GROUPS = POOL // GROUP
+EMB_GROUPS = EMB // GROUP
+TOPIC_GROUPS = TOPICS // GROUP
 CAND_TILES = CANDS // P
-CHUNKS = [(0, 512), (512, 1024)]
-LOADS = ["i0","t0","i1","bs","t1","b0","i2","as","a0","b1","b2","a1","co","ts"]
-CAST_ON_SCALAR = {0: False, 1: True, 2: False}
-ORDER = [
-    ("item", 0, 0),
-    ("item", 0, 1),
-    ("vec",),
-    ("item", 1, 0),
-    ("item", 1, 1),
-    ("map", 0),
-    ("nop",),
-    ("nop",),
-    ("nop",),
-    ("nop",),
-    ("v", 0, 0, 0),
-    ("v", 0, 0, 1),
-    ("v", 0, 0, 2),
-    ("v", 0, 0, 3),
-    ("map", 1),
-    ("bs",),
-    ("v", 0, 1, 0),
-    ("v", 0, 1, 1),
-    ("v", 0, 1, 2),
-    ("v", 0, 1, 3),
-    ("bc", 0),
-    ("item", 2, 0),
-    ("item", 2, 1),
-    ("v", 1, 0, 0),
-    ("v", 1, 0, 1),
-    ("v", 1, 0, 2),
-    ("v", 1, 0, 3),
-    ("bc", 1),
-    ("r", 0, 0, 0),
-    ("r", 0, 0, 1),
-    ("r", 0, 0, 2),
-    ("r", 0, 0, 3),
-    ("bc", 2),
-    ("r", 0, 1, 0),
-    ("v", 0, 2, 0),
-    ("r", 0, 1, 1),
-    ("v", 0, 2, 1),
-    ("r", 0, 1, 2),
-    ("v", 0, 2, 2),
-    ("r", 0, 1, 3),
-    ("v", 0, 2, 3),
-    ("r", 0, 2, 0),
-    ("r", 0, 2, 1),
-    ("r", 0, 2, 2),
-    ("r", 0, 2, 3),
-    ("r", 1, 0, 0),
-    ("r", 1, 0, 1),
-    ("r", 1, 0, 2),
-    ("r", 1, 0, 3),
-    ("r", 1, 1, 0),
-    ("r", 1, 1, 1),
-    ("r", 1, 1, 2),
-    ("r", 1, 1, 3),
-    ("r", 1, 2, 0),
-    ("r", 1, 2, 1),
-    ("r", 1, 2, 2),
-    ("r", 1, 2, 3),
-    ("cost",),
-    ("v", 1, 1, 0),
-    ("v", 1, 1, 1),
-    ("gain", 0, 0),
-    ("v", 1, 1, 2),
-    ("v", 1, 1, 3),
-    ("v", 1, 2, 0),
-    ("v", 1, 2, 1),
-    ("v", 1, 2, 2),
-    ("v", 1, 2, 3),
-    ("gain", 0, 1),
-    ("gain", 0, 2),
-    ("gain", 0, 3),
-    ("gain", 0, 4),
-    ("gain", 0, 5),
-    ("gain", 0, 6),
-    ("gain", 0, 7),
-    ("plane", 0, 0, 2),
-    ("plane", 0, 2, 2),
-    ("gain", 1, 0),
-    ("gain", 1, 1),
-    ("gain", 1, 2),
-    ("gain", 1, 3),
-    ("plane", 0, 4, 2),
-    ("plane", 0, 6, 2),
-    ("gain", 1, 4),
-    ("gain", 1, 5),
-    ("gain", 1, 6),
-    ("gain", 1, 7),
-    ("plane", 1, 0, 2),
-    ("plane", 1, 2, 2),
-    ("nop",),
-    ("plane", 1, 4, 2),
-    ("plane", 1, 6, 1),
-    ("plane", 1, 7, 1),
-]
-RING = 5
-ITEM_COPY_ON_VECTOR = [2]
-CAST_V = [(1, 1), (1, 4), (1, 6), (1, 7), (9, 1, 6)]
-PLANE_V = [(1, 6)]
-LAG = {"drain":3,"mix":7,"quant":9,"cast":6,"plane":5,"item":9,"map":4}
+TILES_PER_HALF = HALF // P
+STAGING = 5
+
+LAG_SMALL = 1
+LAG_DRAIN = 3
+LAG_MAP_QUANT = 2
+LAG_PLANE_QUANT = 5
+LAG_CAST = 6
+LAG_MIX = 7
+LAG_ITEM_QUANT = 8
+LAG_QUANT = 9
+
+R_DRAINS_ON_VECTOR = [(0, 0, 0), (0, 1, 2), (0, 2, 2)]
+CASTS_ON_VECTOR = [(1, 3), (1, 4), (1, 6), (1, 7)]
 
 
 def tile_facility_location_topic_gain_k4_kernel(
@@ -134,328 +49,335 @@ def tile_facility_location_topic_gain_k4_kernel(
     nc = tc.nc
     with ExitStack() as ctx:
         keep = ctx.enter_context(tc.tile_pool(name="keep", bufs=1))
-        ring = ctx.enter_context(tc.tile_pool(name="ring", bufs=RING))
+        ring = ctx.enter_context(tc.tile_pool(name="ring", bufs=STAGING))
         psum = ctx.enter_context(tc.psum_pool(name="psum", bufs=1))
         ctx.enter_context(tc.manual_schedule())
 
         def kept(name, shape, dtype):
             return keep.tile(shape, dtype, name=name, align_bytes=64)
 
-        banks_used = []
+        banks_taken = []
 
         def next_bank(shape, dtype):
-            name = "bank%d" % (len(banks_used) % 8)
-            banks_used.append(name)
+            name = "bank%d" % (len(banks_taken) % BANKS)
+            banks_taken.append(name)
             return psum.tile(shape, dtype, name=name)
 
-        a_codes = [kept("a_codes%d" % h, [P, EMB_PASSES, BANK], U32) for h in range(2)]
-        a_scales = kept("a_scales", [P, EMB_PASSES, CANDS], U8)
-        b_raw = [kept("b_raw%d" % g, [P, EMB_PASSES, 2 * KPASS], U8) for g in range(GROUPS)]
-        b_codes = [kept("b_codes%d" % g, [P, PACK, EMB_PASSES, 2 * P], U8) for g in range(GROUPS)]
-        b_scales_raw = kept("b_scales_raw", [P, EMB_PASSES, POOL], U8)
-        b_scales = kept("b_scales", [P, PACK, EMB_PASSES, GROUPS, P], U8)
-        items = [kept("items%d" % g, [P, PACK, DESC], BF16) for g in range(GROUPS)]
-        item_words = [kept("item_words%d" % g, [P, P, 2 * PACK], F32) for g in range(GROUPS)]
-        item_codes = [kept("item_codes%d" % g, [P, KPASS], U32) for g in range(GROUPS)]
-        item_scales = [kept("item_scales%d" % g, [P, KPASS], U8) for g in range(GROUPS)]
-        map_raw = [kept("map_raw%d" % c, [P, PACK, hi - lo], BF16) for c, (lo, hi) in enumerate(CHUNKS)]
+        def half_cols(h):
+            return slice(HALF * h, HALF * (h + 1))
+
+        def tile_cols(j, count=1):
+            return slice(P * j, P * (j + count))
+
+        a_codes = [kept("a_codes%d" % h, [P, EMB_GROUPS, HALF], U32) for h in range(2)]
+        a_scales = kept("a_scales", [P, EMB_GROUPS, CANDS], U8)
+        b_raw = [kept("b_raw%d" % g, [P, EMB_GROUPS, 2 * GROUP], U8) for g in range(POOL_GROUPS)]
+        b_codes = [kept("b_codes%d" % g, [P, SLOTS, EMB_GROUPS, 2 * P], U8) for g in range(POOL_GROUPS)]
+        b_scales_raw = kept("b_scales_raw", [P, EMB_GROUPS, POOL], U8)
+        b_scales = kept("b_scales", [P, SLOTS, EMB_GROUPS, POOL_GROUPS, P], U8)
+        items = [kept("items%d" % g, [P, SLOTS, DESC], BF16) for g in range(POOL_GROUPS)]
+        item_words = [kept("item_words%d" % g, [P, P, 2 * SLOTS], F32) for g in range(POOL_GROUPS)]
+        item_codes = [kept("item_codes%d" % g, [P, GROUP], U32) for g in range(POOL_GROUPS)]
+        item_scales = [kept("item_scales%d" % g, [P, GROUP], U8) for g in range(POOL_GROUPS)]
+        map_raw = [kept("map_raw%d" % h, [P, SLOTS, HALF], BF16) for h in range(2)]
         map_codes = kept("map_codes", [P, TOPICS], U32)
         map_scales = kept("map_scales", [P, TOPICS], U8)
-        r_codes = [kept("r_codes%d" % g, [P, CANDS], U32) for g in range(GROUPS)]
-        r_scales = [kept("r_scales%d" % g, [P, CANDS], U8) for g in range(GROUPS)]
-        v_codes = [kept("v_codes%d" % g, [P, TOPICS], U32) for g in range(GROUPS)]
-        v_scales = [kept("v_scales%d" % g, [P, TOPICS], U8) for g in range(GROUPS)]
-        vec_raw = kept("vec_raw", [P, KPASS], BF16)
-        vec_rows = kept("vec_rows", [P, PACK, P], BF16)
-        vec_cols = kept("vec_cols", [P, PACK, GROUPS], F32)
+        r_codes = [kept("r_codes%d" % g, [P, CANDS], U32) for g in range(POOL_GROUPS)]
+        r_scales = [kept("r_scales%d" % g, [P, CANDS], U8) for g in range(POOL_GROUPS)]
+        v_codes = [kept("v_codes%d" % g, [P, TOPICS], U32) for g in range(POOL_GROUPS)]
+        v_scales = [kept("v_scales%d" % g, [P, TOPICS], U8) for g in range(POOL_GROUPS)]
+        vec_raw = kept("vec_raw", [P, GROUP], BF16)
+        vec_rows = kept("vec_rows", [P, SLOTS, P], BF16)
+        bias_cols = kept("bias_cols", [P, SLOTS, POOL_GROUPS], F32)
         cost_rows = kept("cost_rows", [P, P], BF16)
         cost_cols = kept("cost_cols", [P, CAND_TILES], F32)
-        neg_cover = kept("neg_cover", [P, PACK, GROUPS], F32)
+        neg_cover = kept("neg_cover", [P, SLOTS, POOL_GROUPS], F32)
         scale_rows = kept("scale_rows", [P, TOPICS], BF16)
         ident = kept("ident", [P, P], F32)
         ident_bf16 = kept("ident_bf16", [P, P], BF16)
         shuffle = kept("shuffle", [P, P], F32)
         y = kept("y", [P, CAND_TILES, TOPICS], F32)
-        y_pairs = kept("y_pairs", [P, CAND_TILES, 2, TOPICS // PACK, 2], BF16)
-        y_words = [kept("y_words%d" % g, [P, CANDS, 2], F32) for g in range(2)]
-        y_codes = [kept("y_codes%d" % g, [P, CANDS], U32) for g in range(2)]
-        y_scales = kept("y_scales", [P, 2, CANDS], U8)
+        y_pairs = kept("y_pairs", [P, CAND_TILES, 2, TOPICS // SLOTS, 2], BF16)
+        y_words = [kept("y_words%d" % g, [P, CANDS, 2], F32) for g in range(TOPIC_GROUPS)]
+        y_codes = [kept("y_codes%d" % g, [P, CANDS], U32) for g in range(TOPIC_GROUPS)]
+        y_scales = kept("y_scales", [P, TOPIC_GROUPS, CANDS], U8)
 
         nc.vector.memset(b_scales_raw[:].bitcast(I32), 0)
         nc.vector.memset(a_scales[:].bitcast(I32), 0)
-        nc.scalar.dma_start(out=vec_raw[0:GROUPS, :], in_=cover.rearrange("(g n) -> g n", g=GROUPS))
-        nc.scalar.dma_start(out=vec_raw[GROUPS : 2 * GROUPS, :], in_=item_bias.rearrange("(g n) -> g n", g=GROUPS))
+        nc.scalar.dma_start(out=vec_raw[0:POOL_GROUPS, :], in_=cover.rearrange("(g n) -> g n", g=POOL_GROUPS))
+        nc.scalar.dma_start(
+            out=vec_raw[POOL_GROUPS : 2 * POOL_GROUPS, :], in_=item_bias.rearrange("(g n) -> g n", g=POOL_GROUPS)
+        )
         make_identity(nc, ident[:])
         nc.gpsimd.memset(vec_rows[:], 0.0)
         nc.gpsimd.memset(cost_rows[:], 0.0)
-
         nc.vector.tensor_copy(
-            out=shuffle[:].rearrange("p (t q h) -> p t q h", t=PACK, h=2),
-            in_=ident[:].rearrange("p (q t h) -> p t q h", t=PACK, h=2),
+            out=shuffle[:].rearrange("p (t q z) -> p t q z", t=SLOTS, z=2),
+            in_=ident[:].rearrange("p (q t z) -> p t q z", t=SLOTS, z=2),
         )
-        cand_rows = cand_words.rearrange("g p n t -> p g (n t)")
-        pool_rows = pool_words.rearrange("g p n -> p g n")
-        map_rows = topic_map.rearrange("(p j) w -> p j w", j=PACK)
 
-        def load_planes(plane, scales):
+        def load_items(g, rows=slice(0, SLOTS)):
+            src = item_desc[GROUP * g : GROUP * (g + 1), :].rearrange("(p j) e -> p j e", j=SLOTS)
+            nc.sync.dma_start(out=items[g][:, rows], in_=src[:, rows])
+
+        def load_map(h):
+            nc.sync.dma_start(out=map_raw[h][:], in_=topic_map.rearrange("(p j) w -> p j w", j=SLOTS)[:, :, half_cols(h)])
+
+        def load_a(h):
+            src = cand_words.rearrange("g p n t -> p g (n t)")[:, :, SLOTS * HALF * h : SLOTS * HALF * (h + 1)]
+            nc.sync.dma_start(out=a_codes[h][:].bitcast(I32), in_=src.bitcast(I32))
+
+        def load_b(g):
+            src = pool_words.rearrange("g p n -> p g n")[:, :, 2 * GROUP * g : 2 * GROUP * (g + 1)]
+            nc.sync.dma_start(out=b_raw[g][:].bitcast(I32), in_=src.bitcast(I32))
+
+        def load_plane(plane, scales):
             rows = scales.rearrange("g q n -> q g n")
-            for quad in range(4):
-                nc.sync.dma_start(out=plane[quad:P:32].bitcast(I32), in_=rows[quad:16:4].bitcast(I32))
+            for r in range(4):
+                nc.sync.dma_start(out=plane[r:P:32].bitcast(I32), in_=rows[r:16:4].bitcast(I32))
 
-        for what in LOADS:
-            if what == "bs":
-                load_planes(b_scales_raw, pool_scales)
-            elif what == "as":
-                load_planes(a_scales, cand_scales)
-            elif what == "co":
-                nc.sync.dma_start(out=cost_rows[0:CAND_TILES, :], in_=cost.rearrange("(j p) -> j p", p=P))
-            elif what == "ts":
-                nc.sync.dma_start(out=scale_rows[:], in_=topic_scale.partition_broadcast(P))
-            elif what[0] == "t":
-                c = int(what[1])
-                nc.sync.dma_start(out=map_raw[c][:], in_=map_rows[:, :, CHUNKS[c][0] : CHUNKS[c][1]])
-            elif what.startswith("a"):
-                h = int(what[1])
-                nc.sync.dma_start(out=a_codes[h][:].bitcast(I32), in_=cand_rows[:, :, 4 * BANK * h : 4 * BANK * (h + 1)].bitcast(I32))
-            elif what.startswith("b"):
-                g = int(what[1])
-                nc.sync.dma_start(out=b_raw[g][:].bitcast(I32), in_=pool_rows[:, :, 2 * KPASS * g : 2 * KPASS * (g + 1)].bitcast(I32))
-            else:
-                g = int(what[1])
-                nc.sync.dma_start(out=items[g][:], in_=item_desc[KPASS * g : KPASS * (g + 1), :].rearrange("(p j) e -> p j e", j=PACK))
+        load_items(0, slice(0, 2))
+        load_items(0, slice(2, 4))
+        load_map(0)
+        load_items(1)
+        load_b(1)
+        load_b(0)
+        load_map(1)
+        load_plane(b_scales_raw, pool_scales)
+        nc.sync.dma_start(out=cost_rows[0:CAND_TILES, :], in_=cost.rearrange("(j p) -> j p", p=P))
+        load_items(2)
+        load_a(0)
+        load_plane(a_scales, cand_scales)
+        load_b(2)
+        load_a(1)
+        nc.sync.dma_start(out=scale_rows[:], in_=topic_scale.partition_broadcast(P))
 
         nc.scalar.activation(out=ident_bf16[:], in_=ident[:], func=ACT.Relu)
-
-        def interleave(dst, src):
-            nc.vector.tensor_copy(
-                out=dst.rearrange("p (c i) t -> p c t i", i=4), in_=src.rearrange("p t (c i) -> p c t i", i=4)
-            )
 
         def quantise(codes, scales, values):
             nc.vector.quantize_mx(out=codes.bitcast(FP8X4), scales=scales, in_=values)
 
-        def sort_b_scales():
-            def act():
+        def mix_and_quantise(rows, codes, scales, mix_lag, quant_lag):
+            mixed = []
+
+            def mix():
+                mixed.append(ring.tile([P, HALF, SLOTS], BF16, name="mixed", align_bytes=64))
                 nc.vector.tensor_copy(
-                    out=b_scales[:].rearrange("p t e g m -> p t (e g m)").bitcast(I32).rearrange("p t (m w) -> p t m w", w=2),
-                    in_=b_scales_raw[:].rearrange("p e n -> p (e n)").bitcast(I32).rearrange("p (m t w) -> p t m w", t=PACK, w=2),
+                    out=mixed[0][:].rearrange("p (c i) t -> p c t i", i=4),
+                    in_=rows[:].rearrange("p t (c i) -> p c t i", i=4),
                 )
-            return [(0, act)]
+
+            def quant():
+                quantise(codes, scales, mixed[0][:].rearrange("p n t -> p (n t)"))
+
+            return [(mix_lag, mix), (quant_lag, quant)]
+
+
+        def sort_by_slot(dst, src, words_per_run):
+            nc.vector.tensor_copy(
+                out=dst.bitcast(I32).rearrange("p t (m w) -> p t m w", w=words_per_run),
+                in_=src.bitcast(I32).rearrange("p (m t w) -> p t m w", t=SLOTS, w=words_per_run),
+            )
+
+        def sort_b_scales():
+            dst = b_scales[:].rearrange("p t e g m -> p t (e g m)")
+            return [(0, lambda: sort_by_slot(dst, b_scales_raw[:].rearrange("p e n -> p (e n)"), RUN // 4))]
 
         def sort_b_codes(g):
-            def act():
-                nc.vector.tensor_copy(
-                    out=b_codes[g][:].rearrange("p t e n -> p t (e n)").bitcast(I32).rearrange("p t (m w) -> p t m w", w=4),
-                    in_=b_raw[g][:].rearrange("p e n -> p (e n)").bitcast(I32).rearrange("p (m t w) -> p t m w", t=PACK, w=4),
-                )
-            return [(0, act)]
+            dst = b_codes[g][:].rearrange("p t e n -> p t (e n)")
+            return [(0, lambda: sort_by_slot(dst, b_raw[g][:].rearrange("p e n -> p (e n)"), 2 * RUN // 4))]
 
-        def vectors():
-            bank = next_bank([P, PACK, P], BF16)
+        def turn_vectors():
+            bank = next_bank([P, SLOTS, P], BF16)
 
             def turn():
                 nc.vector.tensor_copy(
-                    out=vec_rows[0 : 2 * GROUPS].rearrange("p t (q r) -> p t q r", r=8),
-                    in_=vec_raw[0 : 2 * GROUPS].rearrange("p (q t r) -> p t q r", t=PACK, r=8),
+                    out=vec_rows[0 : 2 * POOL_GROUPS].rearrange("p t (q r) -> p t q r", r=RUN),
+                    in_=vec_raw[0 : 2 * POOL_GROUPS].rearrange("p (q t r) -> p t q r", t=SLOTS, r=RUN),
                 )
-                for t in range(PACK):
+                for t in range(SLOTS):
                     nc.tensor.transpose(bank[:, t, :], vec_rows[:, t, :], ident_bf16[:])
 
             def drain():
-                nc.scalar.activation(out=neg_cover[:], in_=bank[:, :, 0:GROUPS], func=ACT.Copy, scale=-1.0)
-                nc.scalar.copy(out=vec_cols[:], in_=bank[:, :, GROUPS : 2 * GROUPS])
-            return [(0, turn), (1, drain)]
+                nc.scalar.activation(out=neg_cover[:], in_=bank[:, :, 0:POOL_GROUPS], func=ACT.Copy, scale=-1.0)
+                nc.scalar.copy(out=bias_cols[:], in_=bank[:, :, POOL_GROUPS : 2 * POOL_GROUPS])
 
-        def costs():
+            return [(0, turn), (LAG_SMALL, drain)]
+
+        def turn_cost():
             bank = next_bank([P, P], BF16)
             return [
                 (0, lambda: nc.tensor.transpose(bank[:], cost_rows[:], ident_bf16[:])),
-                (1, lambda: nc.scalar.copy(out=cost_cols[:], in_=bank[:, 0:CAND_TILES])),
+                (LAG_SMALL, lambda: nc.scalar.copy(out=cost_cols[:], in_=bank[:, 0:CAND_TILES])),
             ]
 
-        def item_bank(g, jp):
-            bank = next_bank([P, PACK, P], F32)
+        def turn_items(g, pair):
+            bank = next_bank([P, SLOTS, P], F32)
             words = items[g][:].bitcast(F32)
 
             def turn():
                 for j in range(2):
                     for u in range(2):
-                        nc.tensor.transpose(bank[:, 2 * j + u, :], words[:, 2 * jp + j, u::2], shuffle[:])
+                        nc.tensor.transpose(bank[:, 2 * j + u, :], words[:, 2 * pair + j, u::2], shuffle[:])
 
             def drain():
-                copy = nc.vector.tensor_copy if g in ITEM_COPY_ON_VECTOR else nc.scalar.copy
-                copy(out=item_words[g][:, :, PACK * jp : PACK * (jp + 1)], in_=bank[:].rearrange("p a n -> p n a"))
+                nc.scalar.copy(
+                    out=item_words[g][:, :, SLOTS * pair : SLOTS * (pair + 1)], in_=bank[:].rearrange("p a n -> p n a")
+                )
 
             def quant():
-                quantise(item_codes[g][:], item_scales[g][:], item_words[g][:].rearrange("p n w -> p (n w)").bitcast(BF16))
-            return [(0, turn), (LAG["drain"], drain)] + ([(LAG["item"], quant)] if jp == 1 else [])
+                values = item_words[g][:].rearrange("p n w -> p (n w)").bitcast(BF16)
+                quantise(item_codes[g][:], item_scales[g][:], values)
 
-        def mix_and_quantise(src, codes, scales, width, mix_lag, quant_lag):
-            mixed = []
+            return [(0, turn), (LAG_DRAIN, drain)] + ([(LAG_ITEM_QUANT, quant)] if pair == 1 else [])
 
-            def mix():
-                mixed.append(ring.tile([P, width, PACK], BF16, name="mixed", align_bytes=64))
-                interleave(mixed[0][:], src())
-            return [(mix_lag, mix), (quant_lag, lambda: quantise(codes, scales, mixed[0][:].rearrange("p n t -> p (n t)")))]
-
-        def map_chunk(c):
-            lo, hi = CHUNKS[c]
-            return mix_and_quantise(lambda: map_raw[c][:], map_codes[:, lo:hi], map_scales[:, lo:hi], hi - lo, 0, LAG["map"])
-
-        def finish(rows, codes, scales, width):
-            return mix_and_quantise(lambda: rows[:], codes, scales, width, LAG["mix"], LAG["quant"])
+        def map_half(h):
+            cols = half_cols(h)
+            return mix_and_quantise(map_raw[h], map_codes[:, cols], map_scales[:, cols], 0, LAG_MAP_QUANT)
 
         staged = {}
-        planes_done = []
+
+        def slot_rows(key, t):
+            if t == 0:
+                staged[key] = ring.tile([P, SLOTS, HALF], BF16, name="rows", align_bytes=64)
+            return staged[key]
 
         def r_bank(h, g, t):
-            bank = next_bank([P, BANK], F32)
-            if t == 0:
-                staged["r", h, g] = ring.tile([P, PACK, BANK], BF16, name="rows", align_bytes=64)
-            rows = staged["r", h, g]
-            cols = slice(BANK * h, BANK * (h + 1))
+            bank = next_bank([P, HALF], F32)
+            rows = slot_rows(("r", h, g), t)
+            cols = half_cols(h)
 
             def multiply():
-                for e in range(EMB_PASSES):
+                for e in range(EMB_GROUPS):
                     nc.tensor.matmul_mx(
                         out=bank[:], lhsT=b_codes[g][:, t, e, :].bitcast(FP4X4), lhsT_scale=b_scales[:, t, e, g, :],
                         rhs=a_codes[h][:, e, :].bitcast(FP8X4), rhs_scale=a_scales[:, e, cols],
-                        start=(e == 0), stop=(e == EMB_PASSES - 1),
+                        start=(e == 0), stop=(e == EMB_GROUPS - 1),
                     )
 
             def drain():
-                nc.scalar.activation(out=rows[:, t, :], in_=bank[:], func=ACT.Relu, bias=neg_cover[:, t, g : g + 1])
-            tail = finish(rows, r_codes[g][:, cols], r_scales[g][:, cols], BANK) if t == PACK - 1 else []
-            return [(0, multiply), (LAG["drain"], drain)] + tail
+                shift = neg_cover[:, t, g : g + 1]
+                if (h, g, t) in R_DRAINS_ON_VECTOR:
+                    nc.vector.tensor_scalar(
+                        out=rows[:, t, :], in0=bank[:], scalar1=shift, scalar2=0.0, op0=ALU.add, op1=ALU.max
+                    )
+                else:
+                    nc.scalar.activation(out=rows[:, t, :], in_=bank[:], func=ACT.Relu, bias=shift)
 
-        def v_bank(c, g, t0):
-            lo, hi = CHUNKS[c]
-            width = hi - lo
-            slots = range(t0, t0 + BANK // width)
-            bank = next_bank([P, len(slots), width], F32)
-            if t0 == 0:
-                staged["v", c, g] = ring.tile([P, PACK, width], BF16, name="rows", align_bytes=64)
-            rows = staged["v", c, g]
+            stages = [(0, multiply), (LAG_DRAIN, drain)]
+            if t == SLOTS - 1:
+                stages.extend(mix_and_quantise(rows, r_codes[g][:, cols], r_scales[g][:, cols], LAG_MIX, LAG_QUANT))
+            return stages
+
+        def v_bank(h, g, t):
+            bank = next_bank([P, HALF], F32)
+            rows = slot_rows(("v", h, g), t)
+            cols = half_cols(h)
 
             def multiply():
-                for t in slots:
-                    nc.tensor.matmul_mx(
-                        out=bank[:, t - t0, :], lhsT=item_codes[g][:, P * t : P * (t + 1)].bitcast(FP8X4),
-                        lhsT_scale=item_scales[g][:, P * t : P * (t + 1)],
-                        rhs=map_codes[:, lo:hi].bitcast(FP8X4), rhs_scale=map_scales[:, lo:hi], start=True, stop=True,
-                    )
-
-            def drain():
-                for t in slots:
-                    nc.scalar.activation(
-                        out=rows[:, t, :], in_=bank[:, t - t0, :], func=ACT.Identity, bias=vec_cols[:, t, g : g + 1]
-                    )
-            tail = finish(rows, v_codes[g][:, lo:hi], v_scales[g][:, lo:hi], width) if slots[-1] == PACK - 1 else []
-            return [(0, multiply), (LAG["drain"], drain)] + tail
-
-        def gain_bank(c, j0):
-            lo, hi = CHUNKS[c]
-            width = hi - lo
-            tiles = range(j0, j0 + BANK // width)
-            bank = next_bank([P, len(tiles), width], F32)
-
-            def multiply():
-                for j in tiles:
-                    for g in range(GROUPS):
-                        nc.tensor.matmul_mx(
-                            out=bank[:, j - j0, :], lhsT=r_codes[g][:, P * j : P * (j + 1)].bitcast(FP8X4),
-                            lhsT_scale=r_scales[g][:, P * j : P * (j + 1)],
-                            rhs=v_codes[g][:, lo:hi].bitcast(FP8X4), rhs_scale=v_scales[g][:, lo:hi],
-                            start=(g == 0), stop=(g == GROUPS - 1),
-                        )
-
-            def drain():
-                for j in tiles:
-                    nc.vector.scalar_tensor_tensor(
-                        out=y[:, j, lo:hi], in0=bank[:, j - j0, :], scalar=cost_cols[:, j : j + 1],
-                        in1=scale_rows[:, lo:hi], op0=ALU.subtract, op1=ALU.mult,
-                    )
-                nc.sync.dma_start(
-                    out=out_0[P * j0 : P * (tiles[-1] + 1), lo:hi].rearrange("(a p) n -> p a n", p=P),
-                    in_=y[:, j0 : tiles[-1] + 1, lo:hi],
+                nc.tensor.matmul_mx(
+                    out=bank[:], lhsT=item_codes[g][:, tile_cols(t)].bitcast(FP8X4), lhsT_scale=item_scales[g][:, tile_cols(t)],
+                    rhs=map_codes[:, cols].bitcast(FP8X4), rhs_scale=map_scales[:, cols], start=True, stop=True,
                 )
 
+            def drain():
+                nc.scalar.activation(out=rows[:, t, :], in_=bank[:], func=ACT.Identity, bias=bias_cols[:, t, g : g + 1])
+
+            stages = [(0, multiply), (LAG_DRAIN, drain)]
+            if t == SLOTS - 1:
+                stages.extend(mix_and_quantise(rows, v_codes[g][:, cols], v_scales[g][:, cols], LAG_MIX, LAG_QUANT))
+            return stages
+
+        def gain_bank(h, j):
+            bank = next_bank([P, HALF], F32)
+            cols = half_cols(h)
+
+            def multiply():
+                for g in range(POOL_GROUPS):
+                    nc.tensor.matmul_mx(
+                        out=bank[:], lhsT=r_codes[g][:, tile_cols(j)].bitcast(FP8X4), lhsT_scale=r_scales[g][:, tile_cols(j)],
+                        rhs=v_codes[g][:, cols].bitcast(FP8X4), rhs_scale=v_scales[g][:, cols],
+                        start=(g == 0), stop=(g == POOL_GROUPS - 1),
+                    )
+
+            def drain():
+                nc.vector.scalar_tensor_tensor(
+                    out=y[:, j, cols], in0=bank[:], scalar=cost_cols[:, j : j + 1], in1=scale_rows[:, cols],
+                    op0=ALU.subtract, op1=ALU.mult,
+                )
+                nc.sync.dma_start(out=out_0[tile_cols(j), cols], in_=y[:, j, cols])
+
             def cast():
-                for j in tiles:
-                    src = y[:, j, lo:hi].rearrange("p (m u e) -> p u m e", u=2, e=2)
-                    dst = y_pairs[:, j, :, lo // PACK : hi // PACK, :]
-                    if (c, j) not in CAST_V if CAST_V is not None else CAST_ON_SCALAR[c]:
-                        nc.scalar.copy(out=dst, in_=src)
-                    else:
-                        nc.vector.tensor_copy(out=dst, in_=src)
-            return [(0, multiply), (LAG["drain"], drain), (LAG["cast"], cast)]
+                copy = nc.vector.tensor_copy if (h, j) in CASTS_ON_VECTOR else nc.scalar.copy
+                copy(out=y_pairs[:, j, :, tile_cols(h), :], in_=y[:, j, cols].rearrange("p (m u e) -> p u m e", u=2, e=2))
+
+            return [(0, multiply), (LAG_DRAIN, drain), (LAG_CAST, cast)]
+
+        planes_done = []
 
         def plane_bank(g, j0, count):
             bank = next_bank([P, 2, count, P], F32)
             words = y_pairs[:].rearrange("p j u m e -> p j u (m e)").bitcast(F32)
-            cols = slice(P * j0, P * (j0 + count))
+            cols = tile_cols(j0, count)
 
             def turn():
                 for a in range(count):
                     for u in range(2):
-                        nc.tensor.transpose(bank[:, u, a, :], words[:, j0 + a, u, P * g : P * (g + 1)], ident[:])
+                        nc.tensor.transpose(bank[:, u, a, :], words[:, j0 + a, u, tile_cols(g)], ident[:])
 
             def drain():
-                copy = nc.vector.tensor_copy if (g, j0) in PLANE_V else nc.scalar.copy
-                copy(out=y_words[g][:, cols, :], in_=bank[:].rearrange("p u a n -> p (a n) u"))
+                nc.scalar.copy(out=y_words[g][:, cols, :], in_=bank[:].rearrange("p u a n -> p (a n) u"))
 
             def quant():
-                quantise(y_codes[g][:, cols], y_scales[:, g, cols], y_words[g][:, cols, :].rearrange("p n u -> p (n u)").bitcast(BF16))
-                half = j0 // 4
+                values = y_words[g][:, cols, :].rearrange("p n u -> p (n u)").bitcast(BF16)
+                quantise(y_codes[g][:, cols], y_scales[:, g, cols], values)
+                half = j0 // TILES_PER_HALF
                 planes_done.extend([(g, half)] * count)
-                if planes_done.count((g, 0)) + planes_done.count((g, 1)) == CAND_TILES:
-                    for quad in range(4):
-                        nc.sync.dma_start(out=out_2[g, quad:16:4, :].bitcast(I32), in_=y_scales[quad:P:32, g, :].bitcast(I32))
-                if g == 1 or planes_done.count((g, half)) == 4:
-                    span = cols if g == 1 else slice(BANK * half, BANK * (half + 1))
+                last_group = g == TOPIC_GROUPS - 1
+                if last_group or planes_done.count((g, half)) == TILES_PER_HALF:
+                    span = cols if last_group else half_cols(half)
                     nc.sync.dma_start(
-                        out=out_1[g].rearrange("p m t -> p (m t)")[:, PACK * span.start : PACK * span.stop].bitcast(I32),
+                        out=out_1[g].rearrange("p m t -> p (m t)")[:, SLOTS * span.start : SLOTS * span.stop].bitcast(I32),
                         in_=y_codes[g][:, span].bitcast(I32),
                     )
-            return [(0, turn), (LAG["drain"], drain), (LAG["plane"], quant)]
+                if len(planes_done) == TOPIC_GROUPS * CAND_TILES:
+                    for r in range(4):
+                        nc.sync.dma_start(
+                            out=out_2.rearrange("g q m -> q g m")[r:16:4].bitcast(I32), in_=y_scales[r:P:32].bitcast(I32)
+                        )
 
-        makers = {"bs": sort_b_scales, "bc": sort_b_codes, "vec": vectors, "cost": costs, "item": item_bank, "map": map_chunk,
-                  "r": r_bank, "v": v_bank, "gain": gain_bank, "plane": plane_bank, "nop": lambda: []}
-        order = ORDER if ORDER else schedule()
+            return [(0, turn), (LAG_DRAIN, drain), (LAG_PLANE_QUANT, quant)]
+
+        def pause():
+            return []
+
+        def group_of(unit, h, g):
+            return [(unit, h, g, t) for t in range(SLOTS)]
+
+        def gains(h, lo, hi):
+            return [(gain_bank, h, j) for j in range(lo, hi)]
+
+        order = [(turn_items, 0, 0), (turn_items, 0, 1), (turn_vectors,), (turn_items, 1, 0), (turn_items, 1, 1)]
+        order += [(map_half, 0)] + [(pause,)] * 3
+        order += group_of(v_bank, 0, 0) + [(map_half, 1), (sort_b_scales,)]
+        order += group_of(v_bank, 0, 1) + [(sort_b_codes, 0)]
+        order += group_of(v_bank, 1, 0) + [(turn_items, 2, 0), (turn_items, 2, 1), (sort_b_codes, 1)]
+        order += group_of(r_bank, 0, 0) + [(sort_b_codes, 2), (turn_cost,)]
+        order += group_of(r_bank, 0, 1)
+        for r_unit, v_unit in zip(group_of(r_bank, 0, 2), group_of(v_bank, 0, 2)):
+            order += [r_unit, v_unit]
+        for g in range(POOL_GROUPS):
+            order += group_of(r_bank, 1, g)
+        last_v = group_of(v_bank, 1, 1) + group_of(v_bank, 1, 2)
+        order += last_v[:3] + gains(0, 0, 1) + last_v[3:] + gains(0, 1, CAND_TILES)
+        order += [(plane_bank, 0, 0, 2), (plane_bank, 0, 2, 2)] + gains(1, 0, 5)
+        order += [(plane_bank, 0, 4, 2), (plane_bank, 0, 6, 2), (plane_bank, 1, 0, 2)] + gains(1, 5, CAND_TILES)
+        order += [(plane_bank, 1, 2, 2)] + [(pause,)] * 2
+        order += [(plane_bank, 1, 4, 2), (plane_bank, 1, 6, 1), (plane_bank, 1, 7, 1)]
+
         pending = []
-        for step in range(len(order) + max(LAG.values())):
+        for step in range(len(order) + LAG_QUANT):
             if step < len(order):
-                pending.extend((step + lag, -lag, act) for lag, act in makers[order[step][0]](*order[step][1:]))
-            for due in sorted([e for e in pending if e[0] == step], key=lambda e: e[1]):
+                pending.extend((step + lag, -lag, action) for lag, action in order[step][0](*order[step][1:]))
+            for due in sorted([entry for entry in pending if entry[0] == step], key=lambda entry: entry[1]):
                 due[2]()
-
-
-def schedule():
-    def r_group(h, g):
-        return [("r", h, g, t) for t in range(PACK)]
-
-    def v_group(c, g):
-        lo, hi = CHUNKS[c]
-        return [("v", c, g, t) for t in range(0, PACK, BANK // (hi - lo))]
-
-    def weave(main, extra, every, offset=0):
-        woven = []
-        rest = list(extra)
-        for i, unit in enumerate(main):
-            woven.append(unit)
-            if i >= offset and (i - offset) % every == every - 1 and rest:
-                woven.append(rest[0])
-                rest = rest[1:]
-        return woven + rest
-
-    order = [("map", 0), ("vec",), ("cost",), ("item", 0, 0), ("item", 0, 1), ("bs",), ("bc", 0)]
-    order += v_group(0, 0) + [("item", 1, 0), ("item", 1, 1)] + r_group(0, 0) + [("bc", 1), ("map", 1)]
-    order += v_group(0, 1) + [("item", 2, 0), ("item", 2, 1)] + r_group(0, 1) + [("bc", 2)]
-    order += v_group(0, 2) + r_group(0, 2) + r_group(1, 0) + [("map", 2)]
-    order += weave(r_group(1, 1) + v_group(1, 0) + r_group(1, 2), [("gain", 0, 0), ("gain", 0, 2)], 4)
-    order += weave(v_group(1, 1) + v_group(1, 2) + v_group(2, 0), [("gain", 0, 4), ("gain", 0, 6)], 4, 2)
-    order += v_group(2, 1)
-    order += weave([("gain", 1, j) for j in range(8)], v_group(2, 2), 1)
-    order += [("plane", 0, 0, 2), ("plane", 0, 2, 2), ("gain", 2, 0), ("gain", 2, 2), ("plane", 0, 4, 2), ("plane", 0, 6, 2)]
-    order += [("gain", 2, 4), ("gain", 2, 6), ("plane", 1, 0, 2), ("plane", 1, 2, 2), ("plane", 1, 4, 2), ("plane", 1, 6, 2)]
-    return order

@@ -104,10 +104,10 @@ def tile_facility_location_topic_gain_k4_kernel(
 
         nc.vector.memset(b_scales_raw[:].bitcast(I32), 0)
         nc.vector.memset(a_scales[:].bitcast(I32), 0)
-        nc.scalar.dma_start(out=vec_raw[0:POOL_GROUPS, :], in_=cover.rearrange("(g n) -> g n", g=POOL_GROUPS))
-        nc.scalar.dma_start(
-            out=vec_raw[POOL_GROUPS : 2 * POOL_GROUPS, :], in_=item_bias.rearrange("(g n) -> g n", g=POOL_GROUPS)
-        )
+        for first, vector in ((0, cover), (POOL_GROUPS, item_bias)):
+            vec_src = vector.rearrange("(g n) -> g n", g=POOL_GROUPS)
+            nc.scalar.dma_start(out=vec_raw[first : first + 2, :], in_=vec_src[0:2])
+            nc.scalar.dma_start(out=vec_raw[first + 2 : first + 3, :], in_=vec_src[2:3])
         make_identity(nc, ident[:])
         nc.gpsimd.memset(vec_rows[:], 0.0)
         nc.gpsimd.memset(cost_rows[:], 0.0)
@@ -342,7 +342,8 @@ def tile_facility_location_topic_gain_k4_kernel(
                     )
                 if len(planes_done) == TOPIC_GROUPS * CAND_TILES:
                     for r in range(4):
-                        nc.sync.dma_start(
+                        queue = nc.scalar if r % 2 == 0 else nc.sync
+                        queue.dma_start(
                             out=out_2.rearrange("g q m -> q g m")[r:16:4].bitcast(I32), in_=y_scales[r:P:32].bitcast(I32)
                         )
 

from contextlib import ExitStack

import concourse.mybir as mybir
from concourse.masks import make_identity

F32 = mybir.dt.float32
BF16 = mybir.dt.bfloat16
U32 = mybir.dt.uint32
I32 = mybir.dt.int32
U8 = mybir.dt.uint8
FP8X4 = mybir.dt.float8_e4m3fn_x4
FP4X4 = mybir.dt.float4_e2m1fn_x4
ACT = mybir.ActivationFunctionType
ALU = mybir.AluOpType

CANDS, EMB, POOL, DESC, TOPICS = 1024, 1024, 1536, 512, 1024
FLOPS = 2 * CANDS * POOL * EMB + 2 * POOL * TOPICS * DESC + 2 * CANDS * TOPICS * POOL

P = 128
SLOTS = 4
GROUP = P * SLOTS
HALF = 512
RUN = 8
BANKS = 8
POOL_GROUPS = POOL // GROUP
EMB_GROUPS = EMB // GROUP
TOPIC_GROUPS = TOPICS // GROUP
CAND_TILES = CANDS // P
TILES_PER_HALF = HALF // P
STAGING = 5

LAG_SMALL = 1
LAG_DRAIN = 3
LAG_MAP_QUANT = 2
LAG_PLANE_QUANT = 5
LAG_CAST = 6
LAG_MIX = 7
LAG_ITEM_QUANT = 8
LAG_QUANT = 9

R_DRAINS_ON_VECTOR = [(0, 0, 0), (0, 1, 2), (0, 2, 2)]
CASTS_ON_VECTOR = [(1, 3), (1, 4), (1, 6), (1, 7)]


def tile_facility_location_topic_gain_k4_kernel(
    tc, cand_words, cand_scales, pool_words, pool_scales, cover, item_desc, topic_map, item_bias, cost, topic_scale,
    out_0, out_1, out_2,
):
    nc = tc.nc
    with ExitStack() as ctx:
        keep = ctx.enter_context(tc.tile_pool(name="keep", bufs=1))
        ring = ctx.enter_context(tc.tile_pool(name="ring", bufs=STAGING))
        psum = ctx.enter_context(tc.psum_pool(name="psum", bufs=1))
        ctx.enter_context(tc.manual_schedule())

        def kept(name, shape, dtype):
            return keep.tile(shape, dtype, name=name, align_bytes=64)

        banks_taken = []

        def next_bank(shape, dtype):
            name = "bank%d" % (len(banks_taken) % BANKS)
            banks_taken.append(name)
            return psum.tile(shape, dtype, name=name)

        def half_cols(h):
            return slice(HALF * h, HALF * (h + 1))

        def tile_cols(j, count=1):
            return slice(P * j, P * (j + count))

        a_codes = [kept("a_codes%d" % h, [P, EMB_GROUPS, HALF], U32) for h in range(2)]
        a_scales = kept("a_scales", [P, EMB_GROUPS, CANDS], U8)
        b_raw = [kept("b_raw%d" % g, [P, EMB_GROUPS, 2 * GROUP], U8) for g in range(POOL_GROUPS)]
        b_codes = [kept("b_codes%d" % g, [P, SLOTS, EMB_GROUPS, 2 * P], U8) for g in range(POOL_GROUPS)]
        b_scales_raw = kept("b_scales_raw", [P, EMB_GROUPS, POOL], U8)
        b_scales = kept("b_scales", [P, SLOTS, EMB_GROUPS, POOL_GROUPS, P], U8)
        items = [kept("items%d" % g, [P, SLOTS, DESC], BF16) for g in range(POOL_GROUPS)]
        item_words = [kept("item_words%d" % g, [P, P, 2 * SLOTS], F32) for g in range(POOL_GROUPS)]
        item_codes = [kept("item_codes%d" % g, [P, GROUP], U32) for g in range(POOL_GROUPS)]
        item_scales = [kept("item_scales%d" % g, [P, GROUP], U8) for g in range(POOL_GROUPS)]
        map_raw = [kept("map_raw%d" % h, [P, SLOTS, HALF], BF16) for h in range(2)]
        map_codes = kept("map_codes", [P, TOPICS], U32)
        map_scales = kept("map_scales", [P, TOPICS], U8)
        r_codes = [kept("r_codes%d" % g, [P, CANDS], U32) for g in range(POOL_GROUPS)]
        r_scales = [kept("r_scales%d" % g, [P, CANDS], U8) for g in range(POOL_GROUPS)]
        v_codes = [kept("v_codes%d" % g, [P, TOPICS], U32) for g in range(POOL_GROUPS)]
        v_scales = [kept("v_scales%d" % g, [P, TOPICS], U8) for g in range(POOL_GROUPS)]
        vec_raw = kept("vec_raw", [P, GROUP], BF16)
        vec_rows = kept("vec_rows", [P, SLOTS, P], BF16)
        bias_cols = kept("bias_cols", [P, SLOTS, POOL_GROUPS], F32)
        cost_rows = kept("cost_rows", [P, P], BF16)
        cost_cols = kept("cost_cols", [P, CAND_TILES], F32)
        neg_cover = kept("neg_cover", [P, SLOTS, POOL_GROUPS], F32)
        scale_rows = kept("scale_rows", [P, TOPICS], BF16)
        ident = kept("ident", [P, P], F32)
        ident_bf16 = kept("ident_bf16", [P, P], BF16)
        shuffle = kept("shuffle", [P, P], F32)
        y = kept("y", [P, CAND_TILES, TOPICS], F32)
        y_pairs = kept("y_pairs", [P, CAND_TILES, 2, TOPICS // SLOTS, 2], BF16)
        y_words = [kept("y_words%d" % g, [P, CANDS, 2], F32) for g in range(TOPIC_GROUPS)]
        y_codes = [kept("y_codes%d" % g, [P, CANDS], U32) for g in range(TOPIC_GROUPS)]
        y_scales = kept("y_scales", [P, TOPIC_GROUPS, CANDS], U8)

        nc.vector.memset(b_scales_raw[:].bitcast(I32), 0)
        nc.vector.memset(a_scales[:].bitcast(I32), 0)
        for first, vector in ((0, cover), (POOL_GROUPS, item_bias)):
            vec_src = vector.rearrange("(g n) -> g n", g=POOL_GROUPS)
            nc.scalar.dma_start(out=vec_raw[first : first + 2, :], in_=vec_src[0:2])
            nc.scalar.dma_start(out=vec_raw[first + 2 : first + 3, :], in_=vec_src[2:3])
        make_identity(nc, ident[:])
        nc.gpsimd.memset(vec_rows[:], 0.0)
        nc.gpsimd.memset(cost_rows[:], 0.0)
        nc.vector.tensor_copy(
            out=shuffle[:].rearrange("p (t q z) -> p t q z", t=SLOTS, z=2),
            in_=ident[:].rearrange("p (q t z) -> p t q z", t=SLOTS, z=2),
        )

        def load_items(g, rows=slice(0, SLOTS)):
            src = item_desc[GROUP * g : GROUP * (g + 1), :].rearrange("(p j) e -> p j e", j=SLOTS)
            nc.sync.dma_start(out=items[g][:, rows], in_=src[:, rows])

        def load_map(h):
            nc.sync.dma_start(out=map_raw[h][:], in_=topic_map.rearrange("(p j) w -> p j w", j=SLOTS)[:, :, half_cols(h)])

        def load_a(h):
            src = cand_words.rearrange("g p n t -> p g (n t)")[:, :, SLOTS * HALF * h : SLOTS * HALF * (h + 1)]
            nc.sync.dma_start(out=a_codes[h][:].bitcast(I32), in_=src.bitcast(I32))

        def load_b(g):
            src = pool_words.rearrange("g p n -> p g n")[:, :, 2 * GROUP * g : 2 * GROUP * (g + 1)]
            nc.sync.dma_start(out=b_raw[g][:].bitcast(I32), in_=src.bitcast(I32))

        def load_plane(plane, scales):
            rows = scales.rearrange("g q n -> q g n")
            for r in range(4):
                nc.sync.dma_start(out=plane[r:P:32].bitcast(I32), in_=rows[r:16:4].bitcast(I32))

        load_items(0, slice(0, 2))
        load_items(0, slice(2, 4))
        load_map(0)
        load_items(1)
        load_b(1)
        load_b(0)
        load_map(1)
        load_plane(b_scales_raw, pool_scales)
        nc.sync.dma_start(out=cost_rows[0:CAND_TILES, :], in_=cost.rearrange("(j p) -> j p", p=P))
        load_items(2)
        load_a(0)
        load_plane(a_scales, cand_scales)
        load_b(2)
        load_a(1)
        nc.sync.dma_start(out=scale_rows[:], in_=topic_scale.partition_broadcast(P))

        nc.scalar.activation(out=ident_bf16[:], in_=ident[:], func=ACT.Relu)

        def quantise(codes, scales, values):
            nc.vector.quantize_mx(out=codes.bitcast(FP8X4), scales=scales, in_=values)

        def mix_and_quantise(rows, codes, scales, mix_lag, quant_lag):
            mixed = []

            def mix():
                mixed.append(ring.tile([P, HALF, SLOTS], BF16, name="mixed", align_bytes=64))
                nc.vector.tensor_copy(
                    out=mixed[0][:].rearrange("p (c i) t -> p c t i", i=4),
                    in_=rows[:].rearrange("p t (c i) -> p c t i", i=4),
                )

            def quant():
                quantise(codes, scales, mixed[0][:].rearrange("p n t -> p (n t)"))

            return [(mix_lag, mix), (quant_lag, quant)]


        def sort_by_slot(dst, src, words_per_run):
            nc.vector.tensor_copy(
                out=dst.bitcast(I32).rearrange("p t (m w) -> p t m w", w=words_per_run),
                in_=src.bitcast(I32).rearrange("p (m t w) -> p t m w", t=SLOTS, w=words_per_run),
            )

        def sort_b_scales():
            dst = b_scales[:].rearrange("p t e g m -> p t (e g m)")
            return [(0, lambda: sort_by_slot(dst, b_scales_raw[:].rearrange("p e n -> p (e n)"), RUN // 4))]

        def sort_b_codes(g):
            dst = b_codes[g][:].rearrange("p t e n -> p t (e n)")
            return [(0, lambda: sort_by_slot(dst, b_raw[g][:].rearrange("p e n -> p (e n)"), 2 * RUN // 4))]

        def turn_vectors():
            bank = next_bank([P, SLOTS, P], BF16)

            def turn():
                nc.vector.tensor_copy(
                    out=vec_rows[0 : 2 * POOL_GROUPS].rearrange("p t (q r) -> p t q r", r=RUN),
                    in_=vec_raw[0 : 2 * POOL_GROUPS].rearrange("p (q t r) -> p t q r", t=SLOTS, r=RUN),
                )
                for t in range(SLOTS):
                    nc.tensor.transpose(bank[:, t, :], vec_rows[:, t, :], ident_bf16[:])

            def drain():
                nc.scalar.activation(out=neg_cover[:], in_=bank[:, :, 0:POOL_GROUPS], func=ACT.Copy, scale=-1.0)
                nc.scalar.copy(out=bias_cols[:], in_=bank[:, :, POOL_GROUPS : 2 * POOL_GROUPS])

            return [(0, turn), (LAG_SMALL, drain)]

        def turn_cost():
            bank = next_bank([P, P], BF16)
            return [
                (0, lambda: nc.tensor.transpose(bank[:], cost_rows[:], ident_bf16[:])),
                (LAG_SMALL, lambda: nc.scalar.copy(out=cost_cols[:], in_=bank[:, 0:CAND_TILES])),
            ]

        def turn_items(g, pair):
            bank = next_bank([P, SLOTS, P], F32)
            words = items[g][:].bitcast(F32)

            def turn():
                for j in range(2):
                    for u in range(2):
                        nc.tensor.transpose(bank[:, 2 * j + u, :], words[:, 2 * pair + j, u::2], shuffle[:])

            def drain():
                nc.scalar.copy(
                    out=item_words[g][:, :, SLOTS * pair : SLOTS * (pair + 1)], in_=bank[:].rearrange("p a n -> p n a")
                )

            def quant():
                values = item_words[g][:].rearrange("p n w -> p (n w)").bitcast(BF16)
                quantise(item_codes[g][:], item_scales[g][:], values)

            return [(0, turn), (LAG_DRAIN, drain)] + ([(LAG_ITEM_QUANT, quant)] if pair == 1 else [])

        def map_half(h):
            cols = half_cols(h)
            return mix_and_quantise(map_raw[h], map_codes[:, cols], map_scales[:, cols], 0, LAG_MAP_QUANT)

        staged = {}

        def slot_rows(key, t):
            if t == 0:
                staged[key] = ring.tile([P, SLOTS, HALF], BF16, name="rows", align_bytes=64)
            return staged[key]

        def r_bank(h, g, t):
            bank = next_bank([P, HALF], F32)
            rows = slot_rows(("r", h, g), t)
            cols = half_cols(h)

            def multiply():
                for e in range(EMB_GROUPS):
                    nc.tensor.matmul_mx(
                        out=bank[:], lhsT=b_codes[g][:, t, e, :].bitcast(FP4X4), lhsT_scale=b_scales[:, t, e, g, :],
                        rhs=a_codes[h][:, e, :].bitcast(FP8X4), rhs_scale=a_scales[:, e, cols],
                        start=(e == 0), stop=(e == EMB_GROUPS - 1),
                    )

            def drain():
                shift = neg_cover[:, t, g : g + 1]
                if (h, g, t) in R_DRAINS_ON_VECTOR:
                    nc.vector.tensor_scalar(
                        out=rows[:, t, :], in0=bank[:], scalar1=shift, scalar2=0.0, op0=ALU.add, op1=ALU.max
                    )
                else:
                    nc.scalar.activation(out=rows[:, t, :], in_=bank[:], func=ACT.Relu, bias=shift)

            stages = [(0, multiply), (LAG_DRAIN, drain)]
            if t == SLOTS - 1:
                stages.extend(mix_and_quantise(rows, r_codes[g][:, cols], r_scales[g][:, cols], LAG_MIX, LAG_QUANT))
            return stages

        def v_bank(h, g, t):
            bank = next_bank([P, HALF], F32)
            rows = slot_rows(("v", h, g), t)
            cols = half_cols(h)

            def multiply():
                nc.tensor.matmul_mx(
                    out=bank[:], lhsT=item_codes[g][:, tile_cols(t)].bitcast(FP8X4), lhsT_scale=item_scales[g][:, tile_cols(t)],
                    rhs=map_codes[:, cols].bitcast(FP8X4), rhs_scale=map_scales[:, cols], start=True, stop=True,
                )

            def drain():
                nc.scalar.activation(out=rows[:, t, :], in_=bank[:], func=ACT.Identity, bias=bias_cols[:, t, g : g + 1])

            stages = [(0, multiply), (LAG_DRAIN, drain)]
            if t == SLOTS - 1:
                stages.extend(mix_and_quantise(rows, v_codes[g][:, cols], v_scales[g][:, cols], LAG_MIX, LAG_QUANT))
            return stages

        def gain_bank(h, j):
            bank = next_bank([P, HALF], F32)
            cols = half_cols(h)

            def multiply():
                for g in range(POOL_GROUPS):
                    nc.tensor.matmul_mx(
                        out=bank[:], lhsT=r_codes[g][:, tile_cols(j)].bitcast(FP8X4), lhsT_scale=r_scales[g][:, tile_cols(j)],
                        rhs=v_codes[g][:, cols].bitcast(FP8X4), rhs_scale=v_scales[g][:, cols],
                        start=(g == 0), stop=(g == POOL_GROUPS - 1),
                    )

            def drain():
                nc.vector.scalar_tensor_tensor(
                    out=y[:, j, cols], in0=bank[:], scalar=cost_cols[:, j : j + 1], in1=scale_rows[:, cols],
                    op0=ALU.subtract, op1=ALU.mult,
                )
                nc.sync.dma_start(out=out_0[tile_cols(j), cols], in_=y[:, j, cols])

            def cast():
                copy = nc.vector.tensor_copy if (h, j) in CASTS_ON_VECTOR else nc.scalar.copy
                copy(out=y_pairs[:, j, :, tile_cols(h), :], in_=y[:, j, cols].rearrange("p (m u e) -> p u m e", u=2, e=2))

            return [(0, multiply), (LAG_DRAIN, drain), (LAG_CAST, cast)]

        planes_done = []

        def plane_bank(g, j0, count):
            bank = next_bank([P, 2, count, P], F32)
            words = y_pairs[:].rearrange("p j u m e -> p j u (m e)").bitcast(F32)
            cols = tile_cols(j0, count)

            def turn():
                for a in range(count):
                    for u in range(2):
                        nc.tensor.transpose(bank[:, u, a, :], words[:, j0 + a, u, tile_cols(g)], ident[:])

            def drain():
                nc.scalar.copy(out=y_words[g][:, cols, :], in_=bank[:].rearrange("p u a n -> p (a n) u"))

            def quant():
                values = y_words[g][:, cols, :].rearrange("p n u -> p (n u)").bitcast(BF16)
                quantise(y_codes[g][:, cols], y_scales[:, g, cols], values)
                half = j0 // TILES_PER_HALF
                planes_done.extend([(g, half)] * count)
                last_group = g == TOPIC_GROUPS - 1
                if last_group or planes_done.count((g, half)) == TILES_PER_HALF:
                    span = cols if last_group else half_cols(half)
                    nc.sync.dma_start(
                        out=out_1[g].rearrange("p m t -> p (m t)")[:, SLOTS * span.start : SLOTS * span.stop].bitcast(I32),
                        in_=y_codes[g][:, span].bitcast(I32),
                    )
                if len(planes_done) == TOPIC_GROUPS * CAND_TILES:
                    for r in range(4):
                        queue = nc.scalar if r % 2 == 0 else nc.sync
                        queue.dma_start(
                            out=out_2.rearrange("g q m -> q g m")[r:16:4].bitcast(I32), in_=y_scales[r:P:32].bitcast(I32)
                        )

            return [(0, turn), (LAG_DRAIN, drain), (LAG_PLANE_QUANT, quant)]

        def pause():
            return []

        def group_of(unit, h, g):
            return [(unit, h, g, t) for t in range(SLOTS)]

        def gains(h, lo, hi):
            return [(gain_bank, h, j) for j in range(lo, hi)]

        order = [(turn_items, 0, 0), (turn_items, 0, 1), (turn_vectors,), (turn_items, 1, 0), (turn_items, 1, 1)]
        order += [(map_half, 0)] + [(pause,)] * 3
        order += group_of(v_bank, 0, 0) + [(map_half, 1), (sort_b_scales,)]
        order += group_of(v_bank, 0, 1) + [(sort_b_codes, 0)]
        order += group_of(v_bank, 1, 0) + [(turn_items, 2, 0), (turn_items, 2, 1), (sort_b_codes, 1)]
        order += group_of(r_bank, 0, 0) + [(sort_b_codes, 2), (turn_cost,)]
        order += group_of(r_bank, 0, 1)
        for r_unit, v_unit in zip(group_of(r_bank, 0, 2), group_of(v_bank, 0, 2)):
            order += [r_unit, v_unit]
        for g in range(POOL_GROUPS):
            order += group_of(r_bank, 1, g)
        last_v = group_of(v_bank, 1, 1) + group_of(v_bank, 1, 2)
        order += last_v[:3] + gains(0, 0, 1) + last_v[3:] + gains(0, 1, CAND_TILES)
        order += [(plane_bank, 0, 0, 2), (plane_bank, 0, 2, 2)] + gains(1, 0, 5)
        order += [(plane_bank, 0, 4, 2), (plane_bank, 0, 6, 2), (plane_bank, 1, 0, 2)] + gains(1, 5, CAND_TILES)
        order += [(plane_bank, 1, 2, 2)] + [(pause,)] * 2
        order += [(plane_bank, 1, 4, 2), (plane_bank, 1, 6, 1), (plane_bank, 1, 7, 1)]

        pending = []
        for step in range(len(order) + LAG_QUANT):
            if step < len(order):
                pending.extend((step + lag, -lag, action) for lag, action in order[step][0](*order[step][1:]))
            for due in sorted([entry for entry in pending if entry[0] == step], key=lambda entry: entry[1]):
                due[2]()
